import numpy as np, ml_dtypes
CORES = [23,119,17,113]
N = 4
import mx_ref
BF = ml_dtypes.bfloat16
def cols(t, e):
    v = np.concatenate([t.reshape(128, -1, 4), np.zeros((128, 1, 4), BF)], axis=1)
    return np.ascontiguousarray(v[:, e]).reshape(128, -1)
def decode(q):
    o = []
    for b in range(4):
        e = np.zeros((128, 128, 4), np.float32); e[np.arange(128), np.arange(128), b] = 1
        o.append(mx_ref.matmul(mx_ref.quantize(e.reshape(128, 512).astype(BF)), q))
    return np.stack(o, axis=2).reshape(128, -1)
def f(rng, *shape):
    return mx_ref.flush((rng.standard_normal(shape, dtype=np.float32) * np.exp2(rng.integers(-2, 3, shape[:-1] + (1,)))).astype(BF))
def wide(rng, *shape, cols=0):
    v = rng.standard_normal(shape, dtype=np.float32) * np.exp2(rng.integers(-12, 13, shape)).astype(np.float32)
    if cols: v *= np.repeat(np.exp2(rng.integers(-cols, cols + 1, shape[:-2] + (1, shape[-1] // 4))) * (rng.random(shape[:-2] + (1, shape[-1] // 4)) > 0.0625), 4, axis=-1).astype(np.float32)
    return mx_ref.flush(v.astype(BF))
T, K = 512, 128
def setup_inputs(rng):
    u = np.zeros((N, 128, 512), BF); u[:, :, :4] = f(rng, N, 128, 4)
    return {"gr": f(rng, N, 128, 4 * T), "u": u}
def raised(rng, chosen):
    d = setup_inputs(rng)
    for r in range(N):
        g = d["gr"][r].astype(np.float32).reshape(128, T, 4)
        sign = np.where(d["u"][r][:, :4].astype(np.float32) < 0, -1, 1).reshape(128, 1, 4) * rng.choice([-1, 1], K).reshape(1, K, 1)
        v = g * np.float32(2.0 ** -8)
        v[:, chosen[r]] = np.abs(g[:, chosen[r]]) * sign
        d["gr"][r] = mx_ref.flush(v.reshape(128, 4 * T).astype(BF))
    return d
def setup_inputs_same(rng):
    d = raised(rng, [rng.permutation(T)[:K]] * N)
    k = rng.permutation(np.concatenate([[12, -12, -11], rng.integers(-12, 13, N - 3)]))
    d["gr"] = mx_ref.flush((d["gr"].astype(np.float32) * np.exp2(k).astype(np.float32).reshape(N, 1, 1)).astype(BF))
    return d
def setup_inputs_apart(rng):
    p = rng.permutation(T)
    return raised(rng, [p[(r * K + np.arange(K)) % T] for r in range(N)])
def setup_inputs_ties(rng):
    d = setup_inputs(rng); n = T // 11
    for r in range(N):
        p = rng.permutation(T)[:11 * n]
        e = np.full(T, -1); e[p] = np.repeat(np.arange(n), 11)
        s = rng.choice([-1, 1], (n, 11)); s[:, 0] = 1; s[:, 1] = -1
        sign = np.ones(T, np.float32); sign[p] = s.reshape(-1)
        d["gr"][r] = (cols(d["gr"][r], e).astype(np.float32).reshape(128, T, 4) * sign.reshape(1, T, 1)).reshape(128, 4 * T).astype(BF)
    return d
def setup_inputs_few(rng):
    d = setup_inputs(rng); p = rng.permutation(N)
    d["u"][p[0]] = 0
    sign = rng.choice([-1, 1], (128, 1, 4))
    d["u"][p[1]][:, :4] = (sign * rng.uniform(1, 4, (128, 1, 4)) * 2.0 ** 28).reshape(128, 4).astype(BF)
    d["gr"][p[1]] = (sign * rng.choice([-1, 1], (1, T, 1)) * rng.uniform(1, 4, (128, T, 4)) * 2.0 ** 28).reshape(128, 4 * T).astype(BF)
    for r in p[2:2 + N // 2]:
        k = rng.permutation(T)[:rng.integers(1, K)]
        e = np.full(T, -1); e[k] = k
        d["gr"][r] = cols(d["gr"][r], e)
    return d
def setup_inputs_spread(rng):
    d = setup_inputs(rng); d["gr"] = wide(rng, N, 128, 4 * T, cols=8); return d
def check_inputs(d):
    return ["u"] if (d["u"][:, :, 4:].astype(np.float32) != 0).any() else []
def reference(gr, u):
    acc = np.zeros((128, T, 4), np.float32); nb = np.zeros((N, K), np.float32); sc = np.zeros((N, 1, K), np.float32)
    er = gr.astype(np.float32).reshape(N, 128, T, 4)
    for s in range(N):
        score = np.abs(mx_ref.matmul(mx_ref.quantize(u[s]), mx_ref.quantize(gr[s]))[0]) + np.float32(0.0)
        e = np.argsort(-score, kind="stable")[:K]
        v = decode(mx_ref.quantize(cols(gr[s], e))).reshape(128, K, 4)
        acc[:, e] = acc[:, e] + v
        er[s][:, e] = er[s][:, e] - v
        nb[s] = e
        sc[s, 0] = score[e]
    return {"acc": np.stack([acc.reshape(128, 4 * T)] * N), "er": er.reshape(N, 128, 4 * T), "nb": np.stack([nb] * N), "sc": sc}

@@ -1,0 +1,436 @@
+from concourse.bass import DstId, RemoteDMATransfer
+from concourse.mybir import dt, AluOpType as A, ActivationFunctionType as F
+
+NR = 4
+K = 128
+ZB = 4
+TW = ZB + 512 * NR
+X4, U8, F32, BF, I32, U16 = "float8_e4m3fn_x4", "uint8", "float32", "bfloat16", "int32", "uint16"
+
+SCRATCH = {
+    "u4": ("sbuf", [128, 16], BF), "grt": ("sbuf", [128, 2048], BF), "urep": ("sbuf", [128, 512], BF),
+    "sel": ("sbuf", [128, 512], BF), "ones": ("sbuf", [128, 512], BF), "ew": ("sbuf", [128, 520], BF),
+    "uq": ("sbuf", [128, 128], X4), "us": ("sbuf", [128, 128], U8),
+    "gq": ("sbuf", [128, 512], X4), "gs": ("sbuf", [128, 512], U8),
+    "eq": ("sbuf", [128, 512], X4), "es": ("sbuf", [128, 512], U8),
+    "psa": ("psum", [128, 2048], F32), "psb": ("psum", [128, 2048], F32),
+    "pi": ("sbuf", [128, 32], I32), "t3": ("sbuf", [128, 32], I32), "uof": ("sbuf", [128, 32], U16),
+    "p4i": ("sbuf", [128, 8], I32), "p16i": ("sbuf", [128, 8], I32),
+    "p4n": ("sbuf", [128, 8], F32), "p16f": ("sbuf", [128, 8], F32), "tz": ("sbuf", [128, 8], F32),
+    "m4": ("sbuf", [128, 128], F32), "m4d": ("sbuf", [128, 128], F32), "mk4": ("sbuf", [128, 128], F32),
+    "rst": ("sbuf", [128, 512], BF), "gi": ("sbuf", [128, 64], BF), "gd": ("sbuf", [128, 64], BF),
+    "sab": ("sbuf", [128, 512], F32), "scol": ("sbuf", [128, 4], F32), "k1": ("sbuf", [128, 512], F32),
+    "cmp": ("sbuf", [128, 2560], BF), "junk": ("sbuf", [128, 2560], BF), "jnk2": ("sbuf", [128, 768], F32),
+    "cna": ("sbuf", [128, 4], F32), "cnb": ("sbuf", [128, 4], F32),
+    "scn": ("sbuf", [128, 384], BF), "rof": ("sbuf", [128, 4], U16),
+    "win": ("sbuf", [128, 512], BF), "win2": ("sbuf", [128, 8, 32], BF), "tr": ("sbuf", [128, 8, 32], BF),
+    "a0": ("sbuf", [128, 8], BF), "a1": ("sbuf", [128, 8], BF), "a2": ("sbuf", [128, 8], BF),
+    "ofs": ("sbuf", [128, 32], U16),
+    "er32": ("sbuf", [128, 2048], F32), "dif": ("sbuf", [128, 512], F32),
+    "tab": ("sbuf", [128, TW], F32), "pw": ("sbuf", [128, 512], BF), "dat": ("sbuf", [128, 512], BF),
+    "pv": ("sbuf", [128, 384], BF), "pvs": ("sbuf", [128, 384], BF), "pof": ("sbuf", [128, 96], U16),
+    "lw": ("sbuf", [128, 512], BF), "lws": ("sbuf", [128, 512], BF), "lof": ("sbuf", [128, 128], U16),
+    "gsum": ("sbuf", [128, 512], F32), "accs": ("sbuf", [128, 2048], F32),
+    "nbl": ("sbuf", [128, 512], F32), "scb": ("sbuf", [128, 128], F32),
+}
+for _s in range(NR):
+    SCRATCH["lst%d" % _s] = ("sbuf", [128, 8], U16)
+    SCRATCH["q%d" % _s] = ("sbuf", [128, 128], X4)
+    SCRATCH["p%d" % _s] = ("sbuf", [128, 128], U8)
+
+PIECES = (544, 544, 480, 480)
+
+SEMAPHORES = (["gp", "ve", "se", "te", "left", "ldu", "lde", "ster", "stnb", "stsc"]
+              + ["ld%d" % i for i in range(4)] + ["sta%d" % i for i in range(len(PIECES))]
+              + ["al%d" % i for i in range(NR)] + ["ac%d" % i for i in range(NR)])
+
+
+def engines_of(src, cores, topo):
+    dsts = [c for c in cores if c != src]
+    off = [c for c in dsts if topo.chip(c) != topo.chip(src)]
+    on = [c for c in dsts if c not in off]
+    plan, used = {}, []
+    for i, c in enumerate(off):
+        e = topo.engines(src, c)
+        n = len(e) // len(off)
+        plan[c] = e[i * n:(i + 1) * n]
+        used += plan[c]
+    width = len(used) // len(off)
+    for c in on:
+        plan[c] = [x for x in topo.engines(src, c) if x not in used][:width]
+        used += plan[c]
+    return plan
+
+
+def rank_program(g, core, T, topo):
+    rank = T.rank_of(core)
+    if rank is None:
+        return
+    queues = {"g": g, "v": g.vector, "s": g.scalar, "t": g.tensor, "y": g.sync}
+    count = {"gp": 0, "ve": 0, "se": 0, "te": 0}
+    own = {"g": "gp", "v": "ve", "s": "se", "t": "te"}
+    seen = {}
+
+    def need(q, *toks):
+        best = {}
+        for tk in toks:
+            best[tk[0]] = max(best.get(tk[0], 0), tk[1])
+        for sem in best:
+            if seen.get((q, sem), 0) < best[sem]:
+                queues[q].wait_ge(T.sem[sem], best[sem])
+                seen[(q, sem)] = best[sem]
+
+    def did(q, ins):
+        sem = own[q]
+        ins.then_inc(T.sem[sem], 1)
+        count[sem] += 1
+        return (sem, count[sem])
+
+    def dma(q, sem, out, in_):
+        queues[q].dma_start(out, in_).then_inc(T.sem[sem], 16)
+        return (sem, 16)
+
+    V, S, TE = g.vector, g.scalar, g.tensor
+    me = rank
+    mates = [s for s in range(NR) if s != me and topo.chip(T.cores[s]) == topo.chip(core)]
+    late = [s for s in range(NR) if s != me and s not in mates]
+    plan = engines_of(core, T.cores, topo)
+    narr = {s: len(engines_of(T.cores[s], T.cores, topo)[core]) for s in range(NR) if s != me}
+
+    ldu = dma("y", "ldu", T.u4[:, 0:4], T.u[:, 0:4])
+    ld = {}
+    for a in range(4):
+        ld[a] = dma("s" if a % 2 == 0 else "y", "ld%d" % a, T.grt[:, 512 * a:512 * a + 512], T.gr[:, 512 * a:512 * a + 512])
+
+    k_pi = did("g", g.iota(T.pi[:, :], [[0, 32]], 0, 1))
+    k_ew0 = did("v", V.memset(T.ew[:, :], 0.0))
+    k_ones = did("v", V.memset(T.ones[:, :], 1.0))
+    need("g", k_ew0, k_ones)
+    k_ew = did("g", g.affine_select(T.ew[:, 4:516:4], T.ones[:, 0:128], [[1, 128]], A.is_equal, 0.0, 0, -1))
+    k_m4 = did("g", g.iota(T.m4[:, :], [[0, 32], [1, 4]], 0, 0, allow_small_or_imprecise_dtypes=True))
+    k_gi = did("g", g.iota(T.gi[:, :], [[128, 4], [1, 16]], -256, 0, allow_small_or_imprecise_dtypes=True))
+    g.dma_start(T.er32[:, :], T.gr[:, :]).then_inc(T.sem.lde, 16)
+    k_er = ("lde", 16)
+
+    need("v", k_pi)
+    c1 = did("v", V.tensor_scalar(T.t3[:, :], T.pi[:, :], 3, None, A.bitwise_and))
+    c2 = did("v", V.tensor_scalar(T.p4i[:, 0:1], T.pi[:, 0:1], 2, 3, A.arith_shift_right, A.bitwise_and))
+    c3 = did("v", V.tensor_scalar(T.p16i[:, 0:1], T.pi[:, 0:1], 112, None, A.bitwise_and))
+    need("v", c1)
+    k_uof = did("v", V.tensor_copy(T.uof[:, :], T.t3[:, :]))
+    need("v", k_ew)
+    k_eq = {}
+    for b in range(4):
+        c = slice(128 * b, 128 * b + 128)
+        k_eq[b] = did("v", V.quantize_mx(T.eq[:, c], T.es[:, c], T.ew[:, 4 - b:516 - b]))
+    need("v", c3)
+    k_p4 = did("v", V.tensor_scalar(T.p4n[:, 0:1], T.p4i[:, 0:1], -1.0, None, A.mult))
+
+    need("v", k_uof, ldu)
+    need("s", k_uof, ldu)
+    u1 = did("v", V.tensor_copy(T.urep[:, 0:256], T.u4[:, 0:4].indirect(T.uof[:, 0:16])))
+    u2 = did("s", S.activation(T.urep[:, 256:512], T.u4[:, 0:4].indirect(T.uof[:, 16:32]), F.Copy))
+
+    k_gq, k_abs, k_scol, k_k1 = {}, {}, {}, {}
+
+    def codes(a):
+        need("v", ld[a])
+        c = slice(128 * a, 128 * a + 128)
+        k_gq[a] = did("v", V.quantize_mx(T.gq[:, c], T.gs[:, c], T.grt[:, 512 * a:512 * a + 512]))
+
+    def score(a):
+        c = slice(128 * a, 128 * a + 128)
+        need("t", k_uq, k_gq[a])
+        o = slice(512 * a, 512 * a + 128)
+        k_row = did("t", TE.matmul_mx(T.psa[:, o], T.uq[:, :], T.us[:, :], T.gq[:, c], T.gs[:, c], True, True))
+        k_col = did("t", TE.matmul_mx(T.psb[:, o], T.gq[:, c], T.gs[:, c], T.uq[:, :], T.us[:, :], True, True))
+        need("s", k_row)
+        k_abs[a] = did("s", S.activation(T.sab[:, c], T.psa[:, o], F.Abs))
+        need("s", k_col)
+        k_scol[a] = did("s", S.activation(T.scol[:, a:a + 1], T.psb[:, 512 * a:512 * a + 1], F.Abs))
+        need("g", k_abs[a])
+        k_k1[a] = did("g", g.affine_select(T.k1[:, c], T.sab[:, c], [[-1, 128]], A.is_gt, -1.0, 0, 1))
+
+    codes(0)
+    need("v", u1, u2)
+    k_uq = did("v", V.quantize_mx(T.uq[:, :], T.us[:, :], T.urep[:, :]))
+    for a in (1, 2, 3):
+        codes(a)
+    for a in range(4):
+        score(a)
+    k_win = did("v", V.memset(T.win[:, 0:128], 0.0))
+    k_p16 = did("v", V.tensor_copy(T.p16f[:, 0:1], T.p16i[:, 0:1]))
+    k_tz = did("v", V.tensor_scalar(T.tz[:, 0:1], T.t3[:, 0:1], 1024.0, None, A.add))
+    k_dat = did("g", g.iota(T.dat[:, :], [[1, 512]], -255, 0, allow_small_or_imprecise_dtypes=True))
+
+    def against(a, lo, hi):
+        at = 640 * a + (lo if lo < 384 else lo + 128)
+        need("v", k_scol[a], k_abs[(hi - 1) // 128])
+        k, n = None, 128 * a
+        if lo < n:
+            m = min(n, hi)
+            k = did("v", V.tensor_scalar(T.cmp[:, at:at + m - lo], T.sab[:, lo:m], T.scol[:, a:a + 1], None, A.is_ge))
+        if n < hi:
+            m = max(n, lo)
+            k = did("v", V.tensor_scalar(T.cmp[:, at + m - lo:at + hi - lo], T.sab[:, m:hi], T.scol[:, a:a + 1], None, A.is_gt))
+        return k
+
+    def ties(a):
+        need("v", k_k1[a])
+        return did("v", V.tensor_scalar(T.cmp[:, 640 * a + 384:640 * a + 512], T.k1[:, 128 * a:128 * a + 128],
+                                        T.scol[:, a:a + 1], None, A.is_equal))
+
+    k_ca = {}
+
+    def first_sum(a, k):
+        need("s", k)
+        o = slice(640 * a, 640 * a + 384)
+        k_ca[a] = did("s", S.activation(T.junk[:, o], T.cmp[:, o], F.Copy, scale=1.0 / 256, accum_out=T.cna[:, a:a + 1]))
+
+    def last_sum(a, k):
+        need("s", k, k_ca[a])
+        return did("s", S.activation(T.jnk2[:, 256 * a:256 * a + 256], T.cmp[:, 640 * a + 384:640 * a + 640], F.Identity,
+                                     bias=T.cna[:, a:a + 1], accum_out=T.cnb[:, a:a + 1]))
+
+    against(0, 0, 256)
+    against(1, 0, 256)
+    k = against(0, 256, 384)
+    first_sum(0, k)
+    k = against(1, 256, 384)
+    first_sum(1, k)
+    k = against(2, 0, 384)
+    first_sum(2, k)
+    for a in range(3):
+        ties(a)
+        k = against(a, 384, 512)
+        k_cb = last_sum(a, k)
+    k1 = against(3, 0, 384)
+    ties(3)
+    k2 = against(3, 384, 512)
+    need("v", k_gi, k_p16)
+    k_gd = did("v", V.tensor_scalar(T.gd[:, :], T.gi[:, :], T.p16f[:, 0:1], None, A.add))
+    need("v", k1)
+    did("v", V.tensor_tensor_scan(T.scn[:, 0:128], T.cmp[:, 1920:2048], T.cmp[:, 2048:2176], 0.0, A.add, A.add))
+    need("v", k2)
+    did("v", V.tensor_tensor_scan(T.scn[:, 128:256], T.cmp[:, 2176:2304], T.cmp[:, 2304:2432], 0.0, A.add, A.add))
+    k3 = did("v", V.tensor_tensor_scan(T.scn[:, 256:320], T.cmp[:, 2432:2496], T.cmp[:, 2496:2560], 0.0, A.add, A.add))
+    need("v", k_cb)
+    did("v", V.tensor_copy(T.rof[:, 0:3], T.cnb[:, 0:3]))
+    need("v", k3)
+    k_r = did("v", V.tensor_scalar(T.rof[:, 3:4], T.scn[:, 127:128], T.scn[:, 255:256], T.scn[:, 319:320], A.add, A.add))
+
+    need("v", k_r, k_win, k_gd)
+    k_w = did("v", V.tensor_copy(T.win[:, 0:512].indirect(T.rof[:, 0:4]), T.gd[:, :]))
+    need("v", k_w)
+    did("v", V.tensor_copy(T.win2[:, :, 0:16], T.win[:, 0:128]))
+    d2 = did("v", V.tensor_copy(T.win2[:, :, 16:32], T.win[:, 0:128]))
+    need("v", d2)
+    k_tr = did("v", V.transpose(T.tr[:, :, :], T.win2[:, :, :]))
+    need("v", k_tr)
+    k_a0 = did("v", V.tensor_tensor(T.a0[:, :], T.tr[:, :, 0], T.tr[:, :, 16], A.add))
+    need("v", k_a0)
+    k_a1 = did("v", V.tensor_tensor(T.a1[0:64, :], T.a0[0:64, :], T.a0[64:128, :], A.add))
+    need("v", k_a1)
+    for b in range(4):
+        k_a2 = did("v", V.tensor_tensor(T.a2[32 * b:32 * b + 32, :], T.a1[0:32, :], T.a1[32:64, :], A.add))
+    lists = [T["lst%d" % s] for s in range(NR)]
+    qs = [T["q%d" % s] for s in range(NR)]
+    ps = [T["p%d" % s] for s in range(NR)]
+    need("v", k_a2)
+    k_lst = did("v", V.tensor_scalar(lists[me][:, :], T.a2[:, :], 256.0, None, A.add))
+    k_of = {}
+    for t in (2, 3, 0, 1):
+        k_of[t] = did("v", V.tensor_scalar(T.ofs[:, 8 * t:8 * t + 8], T.a2[:, :], 4.0, 1024.0 + t, A.mult, A.add))
+    k_sel = {}
+    for t in (0, 1):
+        need("v", k_of[t])
+        k_sel[t] = did("v", V.tensor_copy(T.sel[:, t:512:4], T.grt[:, 0:2048].indirect(T.ofs[:, 8 * t:8 * t + 8])))
+    need("s", k_m4, k_p4)
+    k_md = did("s", S.activation(T.m4d[:, :], T.m4[:, :], F.Abs, bias=T.p4n[:, 0:1]))
+    did("s", S.activation(T.pw[:, :], T.ones[:, :], F.Copy, scale=-256.0))
+    did("s", S.activation(T.rst[:, :], T.ones[:, :], F.Copy))
+    need("s", k_md)
+    did("s", S.activation(T.mk4[:, :], T.m4d[:, :], F.Relu, bias=1.0, scale=-1.0))
+    k_tab = did("s", S.activation(T.tab[:, 0:ZB], T.ones[:, 0:ZB], F.Copy, scale=0.0))
+    need("s", k_tab)
+    k_rst = did("s", S.activation(T.rst[:, 0:512:4], T.ones[:, 0:128], F.Copy, scale=0.0))
+    for t in (2, 3):
+        need("s", k_of[t])
+        k_sel[t] = did("s", S.activation(T.sel[:, t:512:4], T.grt[:, 0:2048].indirect(T.ofs[:, 8 * t:8 * t + 8]), F.Copy))
+    need("v", k_sel[1], k_sel[3])
+    k_q = did("v", V.quantize_mx(qs[me][:, :], ps[me][:, :], T.sel[:, :]))
+
+    sent = [0]
+
+    def send(src, dst, sem):
+        tr = []
+        for c in plan:
+            rid, pid, _ = topo.addr(c)
+            tr.append(RemoteDMATransfer(dst_ids=[DstId(rid=rid, pnc=pid)], dma_engine_mask=sum(1 << e for e in plan[c]),
+                                        remote_sem=T.sem[sem], src=src, dst=dst))
+            sent[0] += len(plan[c])
+        g.remote_dma_fused(tr, local_sem=T.sem.left)
+
+    need("g", k_lst)
+    send(lists[me][:, :], lists[me][:, :], "al%d" % me)
+    need("g", k_q)
+    send(qs[me][:, :].bitcast(dt.uint8), qs[me][:, :].bitcast(dt.uint8), "ac%d" % me)
+    send(ps[me][:, :], ps[me][:, :], "ac%d" % me)
+
+    x, y = late
+    order = [0, 1, 2, 3] if x else [1, 0, 2, 3]
+    place = {s: i for i, s in enumerate(order)}
+
+    def decode(s, bank, *toks):
+        need("t", k_eq[3], *toks)
+        r = {}
+        for b in range(4):
+            r[b] = did("t", TE.matmul_mx(bank[:, 512 * b:512 * b + 128], T.eq[:, 128 * b:128 * b + 128],
+                                         T.es[:, 128 * b:128 * b + 128], qs[s][:, :], ps[s][:, :], True, True))
+        return r
+
+    def column(s, b):
+        o = ZB + 512 * place[s]
+        return T.tab[:, o + b:o + 512:4]
+
+    def keep(s, bank, dec):
+        r = []
+        for b in range(4):
+            need("s", dec[b])
+            r.append(did("s", S.activation(column(s, b), bank[:, 512 * b:512 * b + 128], F.Copy)))
+        return r
+
+    got = {s: ("ac%d" % s, 2 * narr[s]) for s in narr}
+    heard = {s: ("al%d" % s, narr[s]) for s in narr}
+    heard[me] = k_lst
+    k_v = {}
+
+    last = [k_rst]
+
+    def enter(i):
+        need("v", heard[order[i]], k_dat, *last)
+        last[:] = [did("v", V.tensor_copy(T.pw[:, 0:512].indirect(lists[order[i]][:, 0:8]), T.dat[:, 128 * i:128 * i + 128]))]
+
+    def lookup(i):
+        need("v", heard[order[i]], *last)
+        last[:] = [did("v", V.tensor_tensor(T.pv[:, 128 * i - 128:128 * i], T.pw[:, 0:512].indirect(lists[order[i]][:, 0:8]),
+                                            T.mk4[:, 0:128], A.mult))]
+        return last[0]
+
+    def unfold(out, src, n, k):
+        need("v", k, k_rst)
+        return did("v", V.tensor_tensor_scan(out, T.rst[:, 0:n], src, 0.0, A.mult, A.add))
+
+    def offsets(out, src, k):
+        need("v", k, k_tz)
+        return did("v", V.tensor_scalar(out, src, 4.0, T.tz[:, 0:1], A.mult, A.add))
+
+    dec = decode(me, T.psa, k_q, k_abs[3])
+    need("t", k_scol[3])
+    k_sc = did("t", TE.matmul_mx(T.psb[:, 0:128], T.uq[:, :], T.us[:, :], qs[me][:, :], ps[me][:, :], True, True))
+    if order[0] == me:
+        enter(0)
+    k_dif = {}
+    for b in range(4):
+        need("v", dec[b])
+        k_dif[b] = did("v", V.tensor_tensor(T.dif[:, 128 * b:128 * b + 128], T.sel[:, b:512:4],
+                                            T.psa[:, 512 * b:512 * b + 128], A.subtract))
+    k_ers = [k_er]
+
+    def place_er(h):
+        need("v", k_dif[2 * h + 1], *k_ers)
+        k_ers[:] = [did("v", V.tensor_copy(T.er32[:, 0:2048].indirect(T.ofs[:, 16 * h:16 * h + 16]),
+                                           T.dif[:, 256 * h:256 * h + 256]))]
+
+    place_er(0)
+    if order[0] != me:
+        enter(0)
+    place_er(1)
+    kp1 = lookup(1)
+    need("y", *k_ers)
+    ends = [dma("y", "ster", T.er[:, :], T.er32[:, :])]
+    enter(1)
+    ku1 = unfold(T.pvs[:, 0:128], T.pv[:, 0:128], 128, kp1)
+    lookup(2)
+    k_pof1 = offsets(T.pof[:, 0:32], T.pvs[:, 3:128:4], ku1)
+    enter(2)
+    kp3 = lookup(3)
+    enter(3)
+    k_places = last[0]
+    ku2 = unfold(T.pvs[:, 128:384], T.pv[:, 128:384], 256, kp3)
+    k_pof = offsets(T.pof[:, 32:96], T.pvs[:, 131:384:4], ku2)
+
+    k_v[me] = keep(me, T.psa, k_dif)
+    need("s", k_sc)
+    k_scb = did("s", S.activation(T.scb[:, :], T.psb[:, 0:128], F.Abs))
+    need("y", k_scb)
+    ends.append(dma("y", "stsc", T.sc[:, :], T.scb[0:1, :]))
+    prev = [k_scb]
+
+    def gather_first():
+        need("s", k_tab, k_pof1, *k_v[order[0]])
+        return did("s", S.activation(T.gsum[:, :], T.tab[:, 0:ZB + 512].indirect(T.pof[:, 0:32]), F.Copy))
+
+    if order[0] == me:
+        k_gs = gather_first()
+    for s in mates:
+        dec = decode(s, T.psb, got[s], *prev)
+        k_v[s] = keep(s, T.psb, dec)
+        prev = k_v[s]
+    if order[0] != me:
+        k_gs = gather_first()
+
+    def mask():
+        need("s", k_places, k_rst)
+        for i in range(4):
+            k = did("s", S.activation(T.lw[:, i:512:4], T.pw[:, i:512:4], F.Identity, scale=T.mk4[:, i:i + 1]))
+        return k
+
+    dx = decode(x, T.psa, got[x], *k_v[me])
+    dy = decode(y, T.psb, got[y], *prev)
+    early = order[2] != y
+    if early:
+        k_lw = mask()
+    k_v[y] = keep(y, T.psb, dy)
+    if not early:
+        k_lw = mask()
+    need("v", k_gs)
+    total = list(k_v[order[0]])
+    for b in range(4):
+        need("v", dx[b])
+        total.append(did("v", V.tensor_tensor(column(x, b), T.gsum[:, b:512:4], T.psa[:, 512 * b:512 * b + 128], A.add)))
+    if early:
+        ku = unfold(T.lws[:, :], T.lw[:, :], 512, k_lw)
+    for i in (2, 3):
+        need("v", k_pof, *k_v[order[i]], *total)
+        o = T.tab[:, ZB + 512 * i:ZB + 512 * i + 512]
+        total.append(did("v", V.tensor_tensor(o, T.tab[:, 0:ZB + 512 * i].indirect(T.pof[:, 32 * i - 32:32 * i]), o, A.add)))
+        if i == 2 and early:
+            k_lof = offsets(T.lof[:, :], T.lws[:, 3:512:4], ku)
+        if i == 2 and not early:
+            ku = unfold(T.lws[:, :], T.lw[:, :], 512, k_lw)
+    if not early:
+        k_lof = offsets(T.lof[:, :], T.lws[:, 3:512:4], ku)
+    k_nb = None
+    for s in range(NR):
+        need("s", heard[s], k_dat)
+        k_nb = did("s", S.activation(T.nbl[:, 128 * s:128 * s + 128], T.dat[:, 0:512].indirect(lists[s][:, 0:8]), F.Copy,
+                                     bias=255.0))
+    need("y", k_nb)
+    ends.append(dma("y", "stnb", T.nb[:, :], T.nbl[0:1, :]))
+    need("v", k_lof, k_tab, *total)
+    need("s", k_lof, k_tab, *total)
+    at = 0
+    for i, n in enumerate(PIECES):
+        o = T.accs[:, at:at + n]
+        window = T.tab[:, 0:TW].indirect(T.lof[:, at // 16:(at + n) // 16])
+        if i % 2 == 0:
+            k = did("v", V.tensor_copy(o, window))
+        else:
+            k = did("s", S.activation(o, window, F.Copy))
+        need("y", k)
+        ends.append(dma("y", "sta%d" % i, T.acc[:, at:at + n], o))
+        at += n
+
+    need("y", *ends)
+    need("g", ("left", sent[0]), *[(sem, count[sem]) for sem in ("gp", "ve", "se", "te")])

@@ -3,42 +3,42 @@ from concourse.mybir import dt, AluOpType as A, ActivationFunctionType as F
 
 NR = 4
 K = 128
-ZB = 4
-TW = ZB + 512 * NR
-X4, U8, F32, BF, I32, U16 = "float8_e4m3fn_x4", "uint8", "float32", "bfloat16", "int32", "uint16"
+TW = 520
+X4, U8, F32, BF, I32, U16, F16 = "float8_e4m3fn_x4", "uint8", "float32", "bfloat16", "int32", "uint16", "float16"
 
 SCRATCH = {
     "u4": ("sbuf", [128, 16], BF), "grt": ("sbuf", [128, 2048], BF), "urep": ("sbuf", [128, 512], BF),
-    "sel": ("sbuf", [128, 512], BF), "ones": ("sbuf", [128, 512], BF), "ew": ("sbuf", [128, 520], BF),
+    "sel": ("sbuf", [128, 512], BF), "ones": ("sbuf", [128, 128], BF), "ew": ("sbuf", [128, 520], BF),
     "uq": ("sbuf", [128, 128], X4), "us": ("sbuf", [128, 128], U8),
     "gq": ("sbuf", [128, 512], X4), "gs": ("sbuf", [128, 512], U8),
     "eq": ("sbuf", [128, 512], X4), "es": ("sbuf", [128, 512], U8),
+    "qq": ("sbuf", [128, 512], X4), "pp": ("sbuf", [128, 512], U8),
     "psa": ("psum", [128, 2048], F32), "psb": ("psum", [128, 2048], F32),
-    "pi": ("sbuf", [128, 32], I32), "t3": ("sbuf", [128, 32], I32), "uof": ("sbuf", [128, 32], U16),
-    "p4i": ("sbuf", [128, 8], I32), "p16i": ("sbuf", [128, 8], I32),
-    "p4n": ("sbuf", [128, 8], F32), "p16f": ("sbuf", [128, 8], F32), "tz": ("sbuf", [128, 8], F32),
-    "m4": ("sbuf", [128, 128], F32), "m4d": ("sbuf", [128, 128], F32), "mk4": ("sbuf", [128, 128], F32),
-    "rst": ("sbuf", [128, 512], BF), "gi": ("sbuf", [128, 64], BF), "gd": ("sbuf", [128, 64], BF),
+    "pi": ("sbuf", [128, 32], I32),
+    "q16": ("sbuf", [128, 32], I32), "qof": ("sbuf", [128, 32], U16), "qf": ("sbuf", [128, 8], F32),
+    "i32": ("sbuf", [128, 32], BF), "e32": ("sbuf", [128, 32], BF),
+    "b16": ("sbuf", [128, 16], BF), "m16": ("sbuf", [128, 16], BF), "mw": ("sbuf", [128, 512], BF),
+    "mp": ("sbuf", [128, 384], BF), "blk": ("sbuf", [128, 8], F32), "mb": ("sbuf", [128, 8], F32),
+    "gi": ("sbuf", [128, 64], F32), "gd": ("sbuf", [128, 64], BF),
+    "dat": ("sbuf", [128, 128], BF), "num": ("sbuf", [128, 512], BF),
     "sab": ("sbuf", [128, 512], F32), "scol": ("sbuf", [128, 4], F32), "k1": ("sbuf", [128, 512], F32),
-    "cmp": ("sbuf", [128, 2560], BF), "junk": ("sbuf", [128, 2560], BF), "jnk2": ("sbuf", [128, 768], F32),
-    "cna": ("sbuf", [128, 4], F32), "cnb": ("sbuf", [128, 4], F32),
-    "scn": ("sbuf", [128, 384], BF), "rof": ("sbuf", [128, 4], U16),
+    "cmp": ("sbuf", [128, 1792], BF), "sg": ("sbuf", [128, 768], BF), "junk": ("sbuf", [128, 768], BF),
+    "cn": ("sbuf", [128, 4], F32), "scn": ("sbuf", [128, 1280], F16), "rof": ("sbuf", [128, 4], U16),
     "win": ("sbuf", [128, 512], BF), "win2": ("sbuf", [128, 8, 32], BF), "tr": ("sbuf", [128, 8, 32], BF),
     "a0": ("sbuf", [128, 8], BF), "a1": ("sbuf", [128, 8], BF), "a2": ("sbuf", [128, 8], BF),
     "ofs": ("sbuf", [128, 32], U16),
+    "ll": ("sbuf", [128, 32], U16), "xl": ("sbuf", [128, 8], U16),
     "er32": ("sbuf", [128, 2048], F32), "dif": ("sbuf", [128, 512], F32),
-    "tab": ("sbuf", [128, TW], F32), "pw": ("sbuf", [128, 512], BF), "dat": ("sbuf", [128, 512], BF),
-    "pv": ("sbuf", [128, 384], BF), "pvs": ("sbuf", [128, 384], BF), "pof": ("sbuf", [128, 96], U16),
-    "lw": ("sbuf", [128, 512], BF), "lws": ("sbuf", [128, 512], BF), "lof": ("sbuf", [128, 128], U16),
-    "gsum": ("sbuf", [128, 512], F32), "accs": ("sbuf", [128, 2048], F32),
-    "nbl": ("sbuf", [128, 512], F32), "scb": ("sbuf", [128, 128], F32),
+    "tab": ("sbuf", [128, 4, TW], F32), "pw": ("sbuf", [128, 512], BF), "pv": ("sbuf", [128, 384], BF),
+    "un": ("sbuf", [128, 896], F16), "c1": ("sbuf", [128, 56], F16), "c2": ("sbuf", [128, 56], F16),
+    "off": ("sbuf", [128, 56], U16), "gsum": ("sbuf", [128, 12, 128], F32), "accs": ("sbuf", [128, 2048], F32),
+    "nbl": ("sbuf", [128, 128], F32), "scb": ("sbuf", [128, 128], F32),
 }
-for _s in range(NR):
-    SCRATCH["lst%d" % _s] = ("sbuf", [128, 8], U16)
-    SCRATCH["q%d" % _s] = ("sbuf", [128, 128], X4)
-    SCRATCH["p%d" % _s] = ("sbuf", [128, 128], U8)
 
-PIECES = (544, 544, 480, 480)
+EARLY = 2
+PIECES = (96, 160, 160, 96)
+GATHERS = (("s", 0, 0, 4), ("s", 1, 0, 2), ("s", 1, 2, 4), ("v", 2, 0, 1), ("v", 3, 0, 1), ("v", 2, 1, 2), ("v", 3, 1, 2),
+           ("s", 3, 2, 3), ("v", 2, 2, 3), ("s", 3, 3, 4), ("v", 2, 3, 4))
 
 SEMAPHORES = (["gp", "ve", "se", "te", "left", "ldu", "lde", "ster", "stnb", "stsc"]
               + ["ld%d" % i for i in range(4)] + ["sta%d" % i for i in range(len(PIECES))]
@@ -60,6 +60,12 @@ def engines_of(src, cores, topo):
         plan[c] = [x for x in topo.engines(src, c) if x not in used][:width]
         used += plan[c]
     return plan
+
+
+def view_of(r, cores, topo):
+    near = [s for s in range(NR) if s != r and topo.chip(cores[s]) == topo.chip(cores[r])]
+    far = [s for s in range(NR) if s != r and s not in near]
+    return [r] + near + far, ([0, 1, 2, 3] if far[0] else [1, 0, 2, 3])
 
 
 def rank_program(g, core, T, topo):
@@ -92,8 +98,8 @@ def rank_program(g, core, T, topo):
 
     V, S, TE = g.vector, g.scalar, g.tensor
     me = rank
-    mates = [s for s in range(NR) if s != me and topo.chip(T.cores[s]) == topo.chip(core)]
-    late = [s for s in range(NR) if s != me and s not in mates]
+    (_, mate, x, y), order = view_of(me, T.cores, topo)
+    place = {s: i for i, s in enumerate(order)}
     plan = engines_of(core, T.cores, topo)
     narr = {s: len(engines_of(T.cores[s], T.cores, topo)[core]) for s in range(NR) if s != me}
 
@@ -103,33 +109,43 @@ def rank_program(g, core, T, topo):
         ld[a] = dma("s" if a % 2 == 0 else "y", "ld%d" % a, T.grt[:, 512 * a:512 * a + 512], T.gr[:, 512 * a:512 * a + 512])
 
     k_pi = did("g", g.iota(T.pi[:, :], [[0, 32]], 0, 1))
-    k_ew0 = did("v", V.memset(T.ew[:, :], 0.0))
     k_ones = did("v", V.memset(T.ones[:, :], 1.0))
+    k_ew0 = did("v", V.memset(T.ew[:, :], 0.0))
+    k_i32 = did("g", g.iota(T.i32[:, :], [[0, 2], [1, 16]], 0, 0, allow_small_or_imprecise_dtypes=True))
     need("g", k_ew0, k_ones)
     k_ew = did("g", g.affine_select(T.ew[:, 4:516:4], T.ones[:, 0:128], [[1, 128]], A.is_equal, 0.0, 0, -1))
-    k_m4 = did("g", g.iota(T.m4[:, :], [[0, 32], [1, 4]], 0, 0, allow_small_or_imprecise_dtypes=True))
-    k_gi = did("g", g.iota(T.gi[:, :], [[128, 4], [1, 16]], -256, 0, allow_small_or_imprecise_dtypes=True))
+    k_gi = did("g", g.iota(T.gi[:, :], [[128, 4], [1, 16]], -256, 1, allow_small_or_imprecise_dtypes=True))
     g.dma_start(T.er32[:, :], T.gr[:, :]).then_inc(T.sem.lde, 16)
     k_er = ("lde", 16)
 
     need("v", k_pi)
-    c1 = did("v", V.tensor_scalar(T.t3[:, :], T.pi[:, :], 3, None, A.bitwise_and))
-    c2 = did("v", V.tensor_scalar(T.p4i[:, 0:1], T.pi[:, 0:1], 2, 3, A.arith_shift_right, A.bitwise_and))
-    c3 = did("v", V.tensor_scalar(T.p16i[:, 0:1], T.pi[:, 0:1], 112, None, A.bitwise_and))
-    need("v", c1)
-    k_uof = did("v", V.tensor_copy(T.uof[:, :], T.t3[:, :]))
-    need("v", k_ew)
+    k = did("v", V.tensor_scalar(T.q16[:, :], T.pi[:, :], 15, None, A.bitwise_and))
+    need("v", k)
+    k_qf = did("v", V.tensor_copy(T.qf[:, 0:1], T.q16[:, 0:1]))
+    k_qof = did("v", V.tensor_copy(T.qof[:, :], T.q16[:, :]))
+    need("s", k_ones)
+    for s in range(NR):
+        k_blk = did("s", S.activation(T.blk[32 * s:32 * s + 32, 0:1], T.ones[32 * s:32 * s + 32, 0:1], F.Copy,
+                                      scale=128.0 * place[s]))
+    k_win = did("s", S.activation(T.win[:, 0:128], T.ones[:, :], F.Copy, scale=0.0))
+    k_tab = did("s", S.activation(T.tab[:, :, 0], T.ones[:, 0:4], F.Copy, scale=0.0))
+    need("s", k_ew)
+    k_pw = did("s", S.activation(T.pw[:, :], T.ew[:, 0:512], F.Copy, scale=0.0, bias=-256.0))
+    need("v", k_i32, k_qf)
+    k_e32 = did("v", V.tensor_scalar(T.e32[:, :], T.i32[:, :], T.qf[:, 0:1], 512.0, A.is_equal, A.mult))
     k_eq = {}
-    for b in range(4):
+
+    def unit(b):
+        need("v", k_ew)
         c = slice(128 * b, 128 * b + 128)
         k_eq[b] = did("v", V.quantize_mx(T.eq[:, c], T.es[:, c], T.ew[:, 4 - b:516 - b]))
-    need("v", c3)
-    k_p4 = did("v", V.tensor_scalar(T.p4n[:, 0:1], T.p4i[:, 0:1], -1.0, None, A.mult))
 
-    need("v", k_uof, ldu)
-    need("s", k_uof, ldu)
-    u1 = did("v", V.tensor_copy(T.urep[:, 0:256], T.u4[:, 0:4].indirect(T.uof[:, 0:16])))
-    u2 = did("s", S.activation(T.urep[:, 256:512], T.u4[:, 0:4].indirect(T.uof[:, 16:32]), F.Copy))
+    for b in range(EARLY):
+        unit(b)
+
+    need("v", ldu)
+    for t in range(4):
+        k_u = did("v", V.tensor_scalar(T.urep[:, t:512:4], T.ones[:, :], T.u4[:, t:t + 1], None, A.mult))
 
     k_gq, k_abs, k_scol, k_k1 = {}, {}, {}, {}
 
@@ -148,80 +164,85 @@ def rank_program(g, core, T, topo):
         k_abs[a] = did("s", S.activation(T.sab[:, c], T.psa[:, o], F.Abs))
         need("s", k_col)
         k_scol[a] = did("s", S.activation(T.scol[:, a:a + 1], T.psb[:, 512 * a:512 * a + 1], F.Abs))
-        need("g", k_abs[a])
-        k_k1[a] = did("g", g.affine_select(T.k1[:, c], T.sab[:, c], [[-1, 128]], A.is_gt, -1.0, 0, 1))
+        if a % 2:
+            need("g", k_abs[a])
+            c = slice(128 * a - 128, 128 * a + 128)
+            k_k1[a - 1] = k_k1[a] = did("g", g.affine_select(T.k1[:, c], T.sab[:, c], [[0, 2], [-1, 128]], A.is_gt, -1.0,
+                                                             0, 1))
+
+    at = [64 * a * (a + 3) for a in range(4)]
+    up = [0, 384, 640]
+
+    def below(a):
+        need("v", k_scol[a])
+        if a:
+            did("v", V.tensor_scalar(T.cmp[:, at[a]:at[a] + 128 * a], T.sab[:, 0:128 * a], T.scol[:, a:a + 1], None, A.is_ge))
+        o = at[a] + 128 * a
+        did("v", V.tensor_scalar(T.cmp[:, o:o + 128], T.sab[:, 128 * a:128 * a + 128], T.scol[:, a:a + 1], None, A.is_gt))
+
+    def ties(a):
+        need("v", k_k1[a])
+        o = at[a] + 128 * a + 128
+        return did("v", V.tensor_scalar(T.cmp[:, o:o + 128], T.k1[:, 128 * a:128 * a + 128], T.scol[:, a:a + 1], None,
+                                        A.is_equal))
+
+    def signs(a, lo, hi):
+        o = up[a] + lo - 128 * (a + 1)
+        need("s", k_scol[a], k_abs[hi // 128 - 1])
+        return did("s", S.activation(T.sg[:, o:o + hi - lo], T.sab[:, lo:hi], F.Sign, bias=T.scol[:, a:a + 1], scale=-1.0))
+
+    def above(a, k):
+        c = slice(up[a], up[a] + 384 - 128 * a)
+        need("s", k)
+        return did("s", S.activation(T.junk[:, c], T.sg[:, c], F.Relu, scale=-1.0, accum_out=T.cn[:, a:a + 1]))
+
+    def add_up(a, *toks):
+        n = 64 * a + 128
+        need("v", *toks)
+        return did("v", V.tensor_tensor_scan(T.scn[:, 320 * a + 320 - n:320 * a + 320], T.cmp[:, at[a]:at[a] + n],
+                                             T.cmp[:, at[a] + n:at[a] + 2 * n], T.cn[:, a:a + 1] if a < 3 else 0.0,
+                                             A.add, A.add))
 
     codes(0)
-    need("v", u1, u2)
+    need("v", k_u)
     k_uq = did("v", V.quantize_mx(T.uq[:, :], T.us[:, :], T.urep[:, :]))
     for a in (1, 2, 3):
         codes(a)
     for a in range(4):
         score(a)
-    k_win = did("v", V.memset(T.win[:, 0:128], 0.0))
-    k_p16 = did("v", V.tensor_copy(T.p16f[:, 0:1], T.p16i[:, 0:1]))
-    k_tz = did("v", V.tensor_scalar(T.tz[:, 0:1], T.t3[:, 0:1], 1024.0, None, A.add))
-    k_dat = did("g", g.iota(T.dat[:, :], [[1, 512]], -255, 0, allow_small_or_imprecise_dtypes=True))
+    k_b16 = did("v", V.tensor_scalar(T.b16[:, :], T.e32[:, 1:17], -2.0, None, A.mult))
+    need("v", k_blk, k_gi)
+    k_gd = did("v", V.tensor_scalar(T.gd[:, :], T.gi[:, :], T.qf[:, 0:1], None, A.subtract))
+    for i in (1, 2, 3):
+        k_mb = did("v", V.tensor_scalar(T.mb[:, i:i + 1], T.blk[:, 0:1], 128.0 * i, -4096.0, A.is_ge, A.mult))
+    need("v", k_b16)
+    k_m16 = did("v", V.tensor_tensor(T.m16[:, :], T.e32[:, 0:16], T.b16[:, :], A.add))
+    for a in range(4):
+        below(a)
+    k_sg = {a: signs(a, 128 * a + 128, 512) for a in (0, 1)}
+    k_up = {0: above(0, k_sg[0])}
+    k_sg[2] = signs(2, 384, 512)
+    for a in (1, 2):
+        k_up[a] = above(a, k_sg[a])
+    k_tie = {a: ties(a) for a in (0, 1, 3, 2)}
+    k_num = did("g", g.iota(T.num[:, :], [[1, 512]], -256, 0, allow_small_or_imprecise_dtypes=True))
+    add_up(0, k_tie[0], k_up[0])
+    add_up(3, k_tie[3])
+    add_up(1, k_tie[1], k_up[1])
+    k = add_up(2, k_tie[2], k_up[2])
+    spare = list(range(EARLY, 4))
 
-    def against(a, lo, hi):
-        at = 640 * a + (lo if lo < 384 else lo + 128)
-        need("v", k_scol[a], k_abs[(hi - 1) // 128])
-        k, n = None, 128 * a
-        if lo < n:
-            m = min(n, hi)
-            k = did("v", V.tensor_scalar(T.cmp[:, at:at + m - lo], T.sab[:, lo:m], T.scol[:, a:a + 1], None, A.is_ge))
-        if n < hi:
-            m = max(n, lo)
-            k = did("v", V.tensor_scalar(T.cmp[:, at + m - lo:at + hi - lo], T.sab[:, m:hi], T.scol[:, a:a + 1], None, A.is_gt))
-        return k
+    def then(*toks):
+        if spare:
+            unit(spare.pop())
+        need("v", *toks)
 
-    def ties(a):
-        need("v", k_k1[a])
-        return did("v", V.tensor_scalar(T.cmp[:, 640 * a + 384:640 * a + 512], T.k1[:, 128 * a:128 * a + 128],
-                                        T.scol[:, a:a + 1], None, A.is_equal))
+    then(k)
+    k_r = did("v", V.tensor_copy(T.rof[:, :], T.scn[:, 319:1280:320]))
 
-    k_ca = {}
-
-    def first_sum(a, k):
-        need("s", k)
-        o = slice(640 * a, 640 * a + 384)
-        k_ca[a] = did("s", S.activation(T.junk[:, o], T.cmp[:, o], F.Copy, scale=1.0 / 256, accum_out=T.cna[:, a:a + 1]))
-
-    def last_sum(a, k):
-        need("s", k, k_ca[a])
-        return did("s", S.activation(T.jnk2[:, 256 * a:256 * a + 256], T.cmp[:, 640 * a + 384:640 * a + 640], F.Identity,
-                                     bias=T.cna[:, a:a + 1], accum_out=T.cnb[:, a:a + 1]))
-
-    against(0, 0, 256)
-    against(1, 0, 256)
-    k = against(0, 256, 384)
-    first_sum(0, k)
-    k = against(1, 256, 384)
-    first_sum(1, k)
-    k = against(2, 0, 384)
-    first_sum(2, k)
-    for a in range(3):
-        ties(a)
-        k = against(a, 384, 512)
-        k_cb = last_sum(a, k)
-    k1 = against(3, 0, 384)
-    ties(3)
-    k2 = against(3, 384, 512)
-    need("v", k_gi, k_p16)
-    k_gd = did("v", V.tensor_scalar(T.gd[:, :], T.gi[:, :], T.p16f[:, 0:1], None, A.add))
-    need("v", k1)
-    did("v", V.tensor_tensor_scan(T.scn[:, 0:128], T.cmp[:, 1920:2048], T.cmp[:, 2048:2176], 0.0, A.add, A.add))
-    need("v", k2)
-    did("v", V.tensor_tensor_scan(T.scn[:, 128:256], T.cmp[:, 2176:2304], T.cmp[:, 2304:2432], 0.0, A.add, A.add))
-    k3 = did("v", V.tensor_tensor_scan(T.scn[:, 256:320], T.cmp[:, 2432:2496], T.cmp[:, 2496:2560], 0.0, A.add, A.add))
-    need("v", k_cb)
-    did("v", V.tensor_copy(T.rof[:, 0:3], T.cnb[:, 0:3]))
-    need("v", k3)
-    k_r = did("v", V.tensor_scalar(T.rof[:, 3:4], T.scn[:, 127:128], T.scn[:, 255:256], T.scn[:, 319:320], A.add, A.add))
-
-    need("v", k_r, k_win, k_gd)
+    then(k_r, k_win, k_gd)
     k_w = did("v", V.tensor_copy(T.win[:, 0:512].indirect(T.rof[:, 0:4]), T.gd[:, :]))
-    need("v", k_w)
+    then(k_w)
     did("v", V.tensor_copy(T.win2[:, :, 0:16], T.win[:, 0:128]))
     d2 = did("v", V.tensor_copy(T.win2[:, :, 16:32], T.win[:, 0:128]))
     need("v", d2)
@@ -233,11 +254,12 @@ def rank_program(g, core, T, topo):
     need("v", k_a1)
     for b in range(4):
         k_a2 = did("v", V.tensor_tensor(T.a2[32 * b:32 * b + 32, :], T.a1[0:32, :], T.a1[32:64, :], A.add))
-    lists = [T["lst%d" % s] for s in range(NR)]
-    qs = [T["q%d" % s] for s in range(NR)]
-    ps = [T["p%d" % s] for s in range(NR)]
+
+    def listed(i):
+        return T.ll[:, 8 * i:8 * i + 8]
+
     need("v", k_a2)
-    k_lst = did("v", V.tensor_scalar(lists[me][:, :], T.a2[:, :], 256.0, None, A.add))
+    k_lst = did("v", V.tensor_scalar(listed(place[me]), T.a2[:, :], 256.0, None, A.add))
     k_of = {}
     for t in (2, 3, 0, 1):
         k_of[t] = did("v", V.tensor_scalar(T.ofs[:, 8 * t:8 * t + 8], T.a2[:, :], 4.0, 1024.0 + t, A.mult, A.add))
@@ -245,20 +267,17 @@ def rank_program(g, core, T, topo):
     for t in (0, 1):
         need("v", k_of[t])
         k_sel[t] = did("v", V.tensor_copy(T.sel[:, t:512:4], T.grt[:, 0:2048].indirect(T.ofs[:, 8 * t:8 * t + 8])))
-    need("s", k_m4, k_p4)
-    k_md = did("s", S.activation(T.m4d[:, :], T.m4[:, :], F.Abs, bias=T.p4n[:, 0:1]))
-    did("s", S.activation(T.pw[:, :], T.ones[:, :], F.Copy, scale=-256.0))
-    did("s", S.activation(T.rst[:, :], T.ones[:, :], F.Copy))
-    need("s", k_md)
-    did("s", S.activation(T.mk4[:, :], T.m4d[:, :], F.Relu, bias=1.0, scale=-1.0))
-    k_tab = did("s", S.activation(T.tab[:, 0:ZB], T.ones[:, 0:ZB], F.Copy, scale=0.0))
-    need("s", k_tab)
-    k_rst = did("s", S.activation(T.rst[:, 0:512:4], T.ones[:, 0:128], F.Copy, scale=0.0))
+    need("s", k_m16, k_qof)
+    k_mw = did("s", S.activation(T.mw[:, :], T.m16[:, 0:16].indirect(T.qof[:, :]), F.Copy))
     for t in (2, 3):
         need("s", k_of[t])
         k_sel[t] = did("s", S.activation(T.sel[:, t:512:4], T.grt[:, 0:2048].indirect(T.ofs[:, 8 * t:8 * t + 8]), F.Copy))
+    need("s", k_mw, k_mb, k_num)
+    k_dat = did("s", S.activation(T.dat[:, :], T.num[:, 1:129], F.Identity, bias=T.blk[:, 0:1]))
+    for i in (1, 2, 3):
+        k_mp = did("s", S.activation(T.mp[:, 128 * i - 128:128 * i], T.mw[:, 0:128], F.Identity, bias=T.mb[:, i:i + 1]))
     need("v", k_sel[1], k_sel[3])
-    k_q = did("v", V.quantize_mx(qs[me][:, :], ps[me][:, :], T.sel[:, :]))
+    k_q = did("v", V.quantize_mx(T.qq[:, 0:128], T.pp[:, 0:128], T.sel[:, :]))
 
     sent = [0]
 
@@ -266,70 +285,45 @@ def rank_program(g, core, T, topo):
         tr = []
         for c in plan:
             rid, pid, _ = topo.addr(c)
+            slots, theirs = view_of(T.rank_of(c), T.cores, topo)
             tr.append(RemoteDMATransfer(dst_ids=[DstId(rid=rid, pnc=pid)], dma_engine_mask=sum(1 << e for e in plan[c]),
-                                        remote_sem=T.sem[sem], src=src, dst=dst))
+                                        remote_sem=T.sem[sem], src=src, dst=dst(128 * slots.index(me), theirs.index(me))))
             sent[0] += len(plan[c])
         g.remote_dma_fused(tr, local_sem=T.sem.left)
 
     need("g", k_lst)
-    send(lists[me][:, :], lists[me][:, :], "al%d" % me)
+    send(listed(place[me]), lambda c, i: listed(i), "al%d" % me)
     need("g", k_q)
-    send(qs[me][:, :].bitcast(dt.uint8), qs[me][:, :].bitcast(dt.uint8), "ac%d" % me)
-    send(ps[me][:, :], ps[me][:, :], "ac%d" % me)
-
-    x, y = late
-    order = [0, 1, 2, 3] if x else [1, 0, 2, 3]
-    place = {s: i for i, s in enumerate(order)}
-
-    def decode(s, bank, *toks):
-        need("t", k_eq[3], *toks)
-        r = {}
-        for b in range(4):
-            r[b] = did("t", TE.matmul_mx(bank[:, 512 * b:512 * b + 128], T.eq[:, 128 * b:128 * b + 128],
-                                         T.es[:, 128 * b:128 * b + 128], qs[s][:, :], ps[s][:, :], True, True))
-        return r
-
-    def column(s, b):
-        o = ZB + 512 * place[s]
-        return T.tab[:, o + b:o + 512:4]
-
-    def keep(s, bank, dec):
-        r = []
-        for b in range(4):
-            need("s", dec[b])
-            r.append(did("s", S.activation(column(s, b), bank[:, 512 * b:512 * b + 128], F.Copy)))
-        return r
-
+    send(T.qq[:, 0:128].bitcast(dt.uint8), lambda c, i: T.qq[:, c:c + 128].bitcast(dt.uint8), "ac%d" % me)
+    send(T.pp[:, 0:128], lambda c, i: T.pp[:, c:c + 128], "ac%d" % me)
     got = {s: ("ac%d" % s, 2 * narr[s]) for s in narr}
     heard = {s: ("al%d" % s, narr[s]) for s in narr}
     heard[me] = k_lst
-    k_v = {}
 
-    last = [k_rst]
+    def decode(bank, lo, hi, *toks):
+        need("t", *k_eq.values(), *toks)
+        return [did("t", TE.matmul_mx(bank[:, 512 * b:512 * b + hi - lo], T.eq[:, 128 * b:128 * b + 128],
+                                      T.es[:, 128 * b:128 * b + 128], T.qq[:, lo:hi], T.pp[:, lo:hi], True, True))
+                for b in range(4)]
 
-    def enter(i):
-        need("v", heard[order[i]], k_dat, *last)
-        last[:] = [did("v", V.tensor_copy(T.pw[:, 0:512].indirect(lists[order[i]][:, 0:8]), T.dat[:, 128 * i:128 * i + 128]))]
+    def region(i, b):
+        return T.tab[:, b, 1 + 128 * i:129 + 128 * i]
 
-    def lookup(i):
-        need("v", heard[order[i]], *last)
-        last[:] = [did("v", V.tensor_tensor(T.pv[:, 128 * i - 128:128 * i], T.pw[:, 0:512].indirect(lists[order[i]][:, 0:8]),
-                                            T.mk4[:, 0:128], A.mult))]
-        return last[0]
+    kept = {}
 
-    def unfold(out, src, n, k):
-        need("v", k, k_rst)
-        return did("v", V.tensor_tensor_scan(out, T.rst[:, 0:n], src, 0.0, A.mult, A.add))
+    def keep(s, bank, dec):
+        for b in range(4):
+            need("s", dec[b])
+            kept[place[s], b] = did("s", S.activation(region(place[s], b), bank[:, 512 * b:512 * b + 128], F.Copy))
 
-    def offsets(out, src, k):
-        need("v", k, k_tz)
-        return did("v", V.tensor_scalar(out, src, 4.0, T.tz[:, 0:1], A.mult, A.add))
+    def block(s):
+        need("v", heard[s])
+        return did("v", V.tensor_copy(T.xl[32 * s:32 * s + 32, :], T.ll[32 * s:32 * s + 32, 8 * place[s]:8 * place[s] + 8]))
 
-    dec = decode(me, T.psa, k_q, k_abs[3])
+    dec = decode(T.psa, 0, 128, k_q, k_abs[3])
     need("t", k_scol[3])
-    k_sc = did("t", TE.matmul_mx(T.psb[:, 0:128], T.uq[:, :], T.us[:, :], qs[me][:, :], ps[me][:, :], True, True))
-    if order[0] == me:
-        enter(0)
+    k_sc = did("t", TE.matmul_mx(T.psb[:, 0:128], T.uq[:, :], T.us[:, :], T.qq[:, 0:128], T.pp[:, 0:128], True, True))
+    block(me)
     k_dif = {}
     for b in range(4):
         need("v", dec[b])
@@ -337,100 +331,86 @@ def rank_program(g, core, T, topo):
                                             T.psa[:, 512 * b:512 * b + 128], A.subtract))
     k_ers = [k_er]
 
-    def place_er(h):
-        need("v", k_dif[2 * h + 1], *k_ers)
-        k_ers[:] = [did("v", V.tensor_copy(T.er32[:, 0:2048].indirect(T.ofs[:, 16 * h:16 * h + 16]),
-                                           T.dif[:, 256 * h:256 * h + 256]))]
+    def place_er(b):
+        need("v", k_dif[b], *k_ers)
+        k_ers[:] = [did("v", V.tensor_copy(T.er32[:, 0:2048].indirect(T.ofs[:, 8 * b:8 * b + 8]),
+                                           T.dif[:, 128 * b:128 * b + 128]))]
 
     place_er(0)
-    if order[0] != me:
-        enter(0)
-    place_er(1)
-    kp1 = lookup(1)
-    need("y", *k_ers)
-    ends = [dma("y", "ster", T.er[:, :], T.er32[:, :])]
-    enter(1)
-    ku1 = unfold(T.pvs[:, 0:128], T.pv[:, 0:128], 128, kp1)
-    lookup(2)
-    k_pof1 = offsets(T.pof[:, 0:32], T.pvs[:, 3:128:4], ku1)
-    enter(2)
-    kp3 = lookup(3)
-    enter(3)
-    k_places = last[0]
-    ku2 = unfold(T.pvs[:, 128:384], T.pv[:, 128:384], 256, kp3)
-    k_pof = offsets(T.pof[:, 32:96], T.pvs[:, 131:384:4], ku2)
-
-    k_v[me] = keep(me, T.psa, k_dif)
+    keep(me, T.psa, k_dif)
     need("s", k_sc)
     k_scb = did("s", S.activation(T.scb[:, :], T.psb[:, 0:128], F.Abs))
+
+    for s in (mate, x, y):
+        k_xl = block(s)
+    place_er(1)
+    need("v", k_xl, k_pw, k_dat)
+    k_en = did("v", V.tensor_copy(T.pw[:, 0:512].indirect(T.xl[:, :]), T.dat[:, :]))
+    place_er(2)
+    need("s", k_xl)
+    k_nb = did("s", S.activation(T.nbl[:, :], T.num[:, 0:512].indirect(T.xl[:, :]), F.Copy, bias=256.0))
+    need("s", k_en, *heard.values())
+    k_pv = did("s", S.activation(T.pv[:, :], T.pw[:, 0:512].indirect(T.ll[:, 8:32]), F.Copy))
+    need("v", k_mw, k_en)
+    did("v", V.tensor_tensor_scan(T.un[:, 384:896], T.pw[:, :], T.mw[:, :], -1024.0, A.max, A.add))
+    place_er(3)
     need("y", k_scb)
-    ends.append(dma("y", "stsc", T.sc[:, :], T.scb[0:1, :]))
-    prev = [k_scb]
-
-    def gather_first():
-        need("s", k_tab, k_pof1, *k_v[order[0]])
-        return did("s", S.activation(T.gsum[:, :], T.tab[:, 0:ZB + 512].indirect(T.pof[:, 0:32]), F.Copy))
-
-    if order[0] == me:
-        k_gs = gather_first()
-    for s in mates:
-        dec = decode(s, T.psb, got[s], *prev)
-        k_v[s] = keep(s, T.psb, dec)
-        prev = k_v[s]
-    if order[0] != me:
-        k_gs = gather_first()
-
-    def mask():
-        need("s", k_places, k_rst)
-        for i in range(4):
-            k = did("s", S.activation(T.lw[:, i:512:4], T.pw[:, i:512:4], F.Identity, scale=T.mk4[:, i:i + 1]))
-        return k
-
-    dx = decode(x, T.psa, got[x], *k_v[me])
-    dy = decode(y, T.psb, got[y], *prev)
-    early = order[2] != y
-    if early:
-        k_lw = mask()
-    k_v[y] = keep(y, T.psb, dy)
-    if not early:
-        k_lw = mask()
-    need("v", k_gs)
-    total = list(k_v[order[0]])
-    for b in range(4):
-        need("v", dx[b])
-        total.append(did("v", V.tensor_tensor(column(x, b), T.gsum[:, b:512:4], T.psa[:, 512 * b:512 * b + 128], A.add)))
-    if early:
-        ku = unfold(T.lws[:, :], T.lw[:, :], 512, k_lw)
-    for i in (2, 3):
-        need("v", k_pof, *k_v[order[i]], *total)
-        o = T.tab[:, ZB + 512 * i:ZB + 512 * i + 512]
-        total.append(did("v", V.tensor_tensor(o, T.tab[:, 0:ZB + 512 * i].indirect(T.pof[:, 32 * i - 32:32 * i]), o, A.add)))
-        if i == 2 and early:
-            k_lof = offsets(T.lof[:, :], T.lws[:, 3:512:4], ku)
-        if i == 2 and not early:
-            ku = unfold(T.lws[:, :], T.lw[:, :], 512, k_lw)
-    if not early:
-        k_lof = offsets(T.lof[:, :], T.lws[:, 3:512:4], ku)
-    k_nb = None
-    for s in range(NR):
-        need("s", heard[s], k_dat)
-        k_nb = did("s", S.activation(T.nbl[:, 128 * s:128 * s + 128], T.dat[:, 0:512].indirect(lists[s][:, 0:8]), F.Copy,
-                                     bias=255.0))
+    ends = [dma("y", "stsc", T.sc[:, :], T.scb[0:1, :])]
     need("y", k_nb)
-    ends.append(dma("y", "stnb", T.nb[:, :], T.nbl[0:1, :]))
-    need("v", k_lof, k_tab, *total)
-    need("s", k_lof, k_tab, *total)
-    at = 0
-    for i, n in enumerate(PIECES):
-        o = T.accs[:, at:at + n]
-        window = T.tab[:, 0:TW].indirect(T.lof[:, at // 16:(at + n) // 16])
-        if i % 2 == 0:
-            k = did("v", V.tensor_copy(o, window))
-        else:
-            k = did("s", S.activation(o, window, F.Copy))
-        need("y", k)
-        ends.append(dma("y", "sta%d" % i, T.acc[:, at:at + n], o))
-        at += n
+    ends.append(dma("y", "stnb", T.nb[:, :], T.nbl[0:128:32, :]))
+    need("y", *k_ers)
+    ends.append(dma("y", "ster", T.er[:, :], T.er32[:, :]))
+    need("v", k_pv, k_mp)
+    k = did("v", V.tensor_tensor_scan(T.un[:, 0:384], T.pv[:, :], T.mp[:, :], -1024.0, A.max, A.add))
+    need("v", k)
+    k = did("v", V.tensor_tensor(T.c1[0:64, :], T.un[0:64, 15:896:16], T.un[64:128, 15:896:16], A.max))
+    need("v", k)
+    for h in (0, 32):
+        k = did("v", V.tensor_tensor(T.c2[h:h + 32, :], T.c1[0:32, :], T.c1[32:64, :], A.max))
+    need("v", k)
+    for h in (0, 64):
+        k_off = did("v", V.tensor_scalar(T.off[h:h + 64, :], T.c2[0:64, :], T.b16[0:64, 15:16], -256.0, A.subtract, A.add))
+
+    mine = list(kept.values())
+    keep(mate, T.psb, decode(T.psb, 128, 256, got[mate], k_scb))
+    theirs = list(kept.values())
+
+    def copy(q, out, src):
+        return did(q, S.activation(out, src, F.Copy) if q == "s" else V.tensor_copy(out, src))
+
+    def window(i, b):
+        return T.tab[:, b, 0:1 + 128 * i].indirect(T.off[:, 8 * i - 8:8 * i])
+
+    fetched = {}
+    for b in range(4):
+        q = "vvss"[b]
+        need(q, k_off, k_tab, kept[0, b])
+        fetched[b] = copy(q, T.gsum[:, b, :], window(1, b))
+    dx = decode(T.psa, 256, 384, got[x], *mine)
+    keep(y, T.psb, decode(T.psb, 384, 512, got[y], *theirs))
+
+    summed = {}
+    for b in range(4):
+        need("v", fetched[b], dx[b])
+        summed[b] = did("v", V.tensor_tensor(region(1, b), T.gsum[:, b, :], T.psa[:, 512 * b:512 * b + 128], A.add))
+    for pair in ((0, 1), (2, 3)):
+        for i in (2, 3):
+            for b in pair:
+                need("v", kept[i, b], summed[b])
+                summed[b] = did("v", V.tensor_tensor(region(i, b), window(i, b), region(i, b), A.add))
+
+    edges = [sum(PIECES[:i]) for i in range(len(PIECES) + 1)]
+    done = {i: [] for i in range(len(PIECES))}
+    for q, b, i, j in GATHERS:
+        lo, hi = edges[i], edges[j]
+        need(q, summed[b])
+        k = copy(q, T.accs[:, 4 * lo + b:4 * hi:4], T.tab[:, b, 0:513].indirect(T.off[:, 24 + lo // 16:24 + hi // 16]))
+        for n in range(i, j):
+            done[n].append(k)
+    for i in done:
+        need("y", *done[i])
+        c = slice(4 * edges[i], 4 * edges[i + 1])
+        ends.append(dma("y", "sta%d" % i, T.acc[:, c], T.accs[:, c]))
 
     need("y", *ends)
     need("g", ("left", sent[0]), *[(sem, count[sem]) for sem in ("gp", "ve", "se", "te")])

@@ -18,7 +18,7 @@ SCRATCH = {
     "q16": ("sbuf", [128, 32], I32), "qof": ("sbuf", [128, 32], U16), "qf": ("sbuf", [128, 8], F32),
     "i32": ("sbuf", [128, 32], BF), "e32": ("sbuf", [128, 32], BF),
     "b16": ("sbuf", [128, 16], BF), "m16": ("sbuf", [128, 16], BF), "mw": ("sbuf", [128, 512], BF),
-    "mp": ("sbuf", [128, 384], BF), "blk": ("sbuf", [128, 8], F32), "mb": ("sbuf", [128, 8], F32),
+    "mp": ("sbuf", [128, 256], BF), "blk": ("sbuf", [128, 8], F32), "mb": ("sbuf", [128, 8], F32),
     "gi": ("sbuf", [128, 64], F32), "gd": ("sbuf", [128, 64], BF),
     "dat": ("sbuf", [128, 128], BF), "num": ("sbuf", [128, 512], BF),
     "sab": ("sbuf", [128, 512], F32), "scol": ("sbuf", [128, 4], F32), "k1": ("sbuf", [128, 512], F32),
@@ -30,12 +30,12 @@ SCRATCH = {
     "ll": ("sbuf", [128, 32], U16), "xl": ("sbuf", [128, 8], U16),
     "er32": ("sbuf", [128, 2048], F32), "dif": ("sbuf", [128, 512], F32),
     "tab": ("sbuf", [128, 4, TW], F32), "pw": ("sbuf", [128, 512], BF), "pv": ("sbuf", [128, 384], BF),
-    "un": ("sbuf", [128, 896], F16), "c1": ("sbuf", [128, 56], F16), "c2": ("sbuf", [128, 56], F16),
-    "off": ("sbuf", [128, 56], U16), "gsum": ("sbuf", [128, 12, 128], F32), "accs": ("sbuf", [128, 2048], F32),
+    "un": ("sbuf", [128, 896], F16), "c1": ("sbuf", [128, 48], F16), "c2": ("sbuf", [128, 48], F16),
+    "off": ("sbuf", [128, 56], U16), "gsum": ("sbuf", [128, 4, 128], F32), "accs": ("sbuf", [128, 2048], F32),
     "nbl": ("sbuf", [128, 128], F32), "scb": ("sbuf", [128, 128], F32),
 }
 
-EARLY = 2
+EARLY = 1
 PIECES = (96, 160, 160, 96)
 GATHERS = (("s", 0, 0, 4), ("s", 1, 0, 2), ("s", 1, 2, 4), ("v", 2, 0, 1), ("v", 3, 0, 1), ("v", 2, 1, 2), ("v", 3, 1, 2),
            ("s", 3, 2, 3), ("v", 2, 2, 3), ("s", 3, 3, 4), ("v", 2, 3, 4))
@@ -213,22 +213,25 @@ def rank_program(g, core, T, topo):
     k_b16 = did("v", V.tensor_scalar(T.b16[:, :], T.e32[:, 1:17], -2.0, None, A.mult))
     need("v", k_blk, k_gi)
     k_gd = did("v", V.tensor_scalar(T.gd[:, :], T.gi[:, :], T.qf[:, 0:1], None, A.subtract))
-    for i in (1, 2, 3):
+    for i in (2, 3):
         k_mb = did("v", V.tensor_scalar(T.mb[:, i:i + 1], T.blk[:, 0:1], 128.0 * i, -4096.0, A.is_ge, A.mult))
     need("v", k_b16)
     k_m16 = did("v", V.tensor_tensor(T.m16[:, :], T.e32[:, 0:16], T.b16[:, :], A.add))
     for a in range(4):
         below(a)
-    k_sg = {a: signs(a, 128 * a + 128, 512) for a in (0, 1)}
+    signs(0, 128, 384)
+    k_sg = {0: signs(0, 384, 512), 1: signs(1, 256, 512)}
     k_up = {0: above(0, k_sg[0])}
     k_sg[2] = signs(2, 384, 512)
     for a in (1, 2):
         k_up[a] = above(a, k_sg[a])
-    k_tie = {a: ties(a) for a in (0, 1, 3, 2)}
-    k_num = did("g", g.iota(T.num[:, :], [[1, 512]], -256, 0, allow_small_or_imprecise_dtypes=True))
+    k_tie = {a: ties(a) for a in (0, 1)}
     add_up(0, k_tie[0], k_up[0])
-    add_up(3, k_tie[3])
+    for a in (3, 2):
+        k_tie[a] = ties(a)
+    k_num = did("g", g.iota(T.num[:, :], [[1, 512]], -256, 0, allow_small_or_imprecise_dtypes=True))
     add_up(1, k_tie[1], k_up[1])
+    add_up(3, k_tie[3])
     k = add_up(2, k_tie[2], k_up[2])
     spare = list(range(EARLY, 4))
 
@@ -274,8 +277,9 @@ def rank_program(g, core, T, topo):
         k_sel[t] = did("s", S.activation(T.sel[:, t:512:4], T.grt[:, 0:2048].indirect(T.ofs[:, 8 * t:8 * t + 8]), F.Copy))
     need("s", k_mw, k_mb, k_num)
     k_dat = did("s", S.activation(T.dat[:, :], T.num[:, 1:129], F.Identity, bias=T.blk[:, 0:1]))
-    for i in (1, 2, 3):
-        k_mp = did("s", S.activation(T.mp[:, 128 * i - 128:128 * i], T.mw[:, 0:128], F.Identity, bias=T.mb[:, i:i + 1]))
+    for i in (2, 3):
+        k_mp = did("s", S.activation(T.mp[:, 128 * i - 256:128 * i - 128], T.mw[:, 0:128], F.Identity,
+                                     bias=T.mb[:, i:i + 1]))
     need("v", k_sel[1], k_sel[3])
     k_q = did("v", V.quantize_mx(T.qq[:, 0:128], T.pp[:, 0:128], T.sel[:, :]))
 
@@ -341,6 +345,16 @@ def rank_program(g, core, T, topo):
     need("s", k_sc)
     k_scb = did("s", S.activation(T.scb[:, :], T.psb[:, 0:128], F.Abs))
 
+    def unfold(out, src, pattern, *toks):
+        need("v", *toks)
+        return did("v", V.tensor_tensor_scan(out, src, pattern, -1024.0, A.max, A.add))
+
+    def copy(q, out, src):
+        return did(q, S.activation(out, src, F.Copy) if q == "s" else V.tensor_copy(out, src))
+
+    def window(i, b):
+        return T.tab[:, b, 0:1 + 128 * i].indirect(T.off[:, 8 * i - 8:8 * i])
+
     for s in (mate, x, y):
         k_xl = block(s)
     place_er(1)
@@ -350,53 +364,61 @@ def rank_program(g, core, T, topo):
     need("s", k_xl)
     k_nb = did("s", S.activation(T.nbl[:, :], T.num[:, 0:512].indirect(T.xl[:, :]), F.Copy, bias=256.0))
     need("s", k_en, *heard.values())
-    k_pv = did("s", S.activation(T.pv[:, :], T.pw[:, 0:512].indirect(T.ll[:, 8:32]), F.Copy))
-    need("v", k_mw, k_en)
-    did("v", V.tensor_tensor_scan(T.un[:, 384:896], T.pw[:, :], T.mw[:, :], -1024.0, A.max, A.add))
+    k_pv = did("s", S.activation(T.pv[:, 128:384], T.pw[:, 0:512].indirect(T.ll[:, 16:32]), F.Copy))
+    need("v", k_en)
+    k = did("v", V.tensor_copy(T.pv[:, 0:128], T.pw[:, 0:512].indirect(listed(1))))
+    unfold(T.un[:, 384:896], T.pw[:, :], T.mw[:, :], k_mw)
+    k = unfold(T.un[:, 0:128], T.pv[:, 0:128], T.mw[:, 0:128], k)
     place_er(3)
+    need("v", k)
+    first = slice(32 * order[0], 32 * order[0] + 32)
+    for h in range(0, 128, 32):
+        k_off1 = did("v", V.tensor_scalar(T.off[h:h + 32, 0:8], T.un[first, 15:128:16], T.b16[first, 15:16], -256.0,
+                                          A.subtract, A.add))
+    k = unfold(T.un[:, 128:384], T.pv[:, 128:384], T.mp[:, :], k_pv, k_mp)
     need("y", k_scb)
     ends = [dma("y", "stsc", T.sc[:, :], T.scb[0:1, :])]
     need("y", k_nb)
     ends.append(dma("y", "stnb", T.nb[:, :], T.nbl[0:128:32, :]))
     need("y", *k_ers)
     ends.append(dma("y", "ster", T.er[:, :], T.er32[:, :]))
-    need("v", k_pv, k_mp)
-    k = did("v", V.tensor_tensor_scan(T.un[:, 0:384], T.pv[:, :], T.mp[:, :], -1024.0, A.max, A.add))
-    need("v", k)
-    k = did("v", V.tensor_tensor(T.c1[0:64, :], T.un[0:64, 15:896:16], T.un[64:128, 15:896:16], A.max))
-    need("v", k)
-    for h in (0, 32):
-        k = did("v", V.tensor_tensor(T.c2[h:h + 32, :], T.c1[0:32, :], T.c1[32:64, :], A.max))
-    need("v", k)
-    for h in (0, 64):
-        k_off = did("v", V.tensor_scalar(T.off[h:h + 64, :], T.c2[0:64, :], T.b16[0:64, 15:16], -256.0, A.subtract, A.add))
 
     mine = list(kept.values())
     keep(mate, T.psb, decode(T.psb, 128, 256, got[mate], k_scb))
     theirs = list(kept.values())
+    fetched, summed = {}, {}
 
-    def copy(q, out, src):
-        return did(q, S.activation(out, src, F.Copy) if q == "s" else V.tensor_copy(out, src))
-
-    def window(i, b):
-        return T.tab[:, b, 0:1 + 128 * i].indirect(T.off[:, 8 * i - 8:8 * i])
-
-    fetched = {}
-    for b in range(4):
-        q = "vvss"[b]
-        need(q, k_off, k_tab, kept[0, b])
+    def fetch(q, b):
+        need(q, k_off1, k_tab, kept[0, b])
         fetched[b] = copy(q, T.gsum[:, b, :], window(1, b))
-    dx = decode(T.psa, 256, 384, got[x], *mine)
-    keep(y, T.psb, decode(T.psb, 384, 512, got[y], *theirs))
 
-    summed = {}
-    for b in range(4):
+    def add(b):
         need("v", fetched[b], dx[b])
         summed[b] = did("v", V.tensor_tensor(region(1, b), T.gsum[:, b, :], T.psa[:, 512 * b:512 * b + 128], A.add))
+
+    for b in (1, 2, 3):
+        fetch("s", b)
+    dx = decode(T.psa, 256, 384, got[x], *mine)
+    keep(y, T.psb, decode(T.psb, 384, 512, got[y], *theirs))
+    fetch("v", 0)
+    need("v", k)
+    k = did("v", V.tensor_tensor(T.c1[0:64, :], T.un[0:64, 143:896:16], T.un[64:128, 143:896:16], A.max))
+    add(0)
+    need("v", k)
+    for h in (0, 32):
+        k = did("v", V.tensor_tensor(T.c2[h:h + 32, :], T.c1[0:32, :], T.c1[32:64, :], A.max))
+    add(1)
+    need("v", k)
+    for h in (0, 64):
+        k_off = did("v", V.tensor_scalar(T.off[h:h + 64, 8:56], T.c2[0:64, :], T.b16[0:64, 15:16], -256.0, A.subtract,
+                                         A.add))
+    add(2)
+    add(3)
+
     for pair in ((0, 1), (2, 3)):
         for i in (2, 3):
             for b in pair:
-                need("v", kept[i, b], summed[b])
+                need("v", k_off, kept[i, b], summed[b])
                 summed[b] = did("v", V.tensor_tensor(region(i, b), window(i, b), region(i, b), A.add))
 
     edges = [sum(PIECES[:i]) for i in range(len(PIECES) + 1)]

@@ -3,7 +3,9 @@ from concourse.mybir import dt, AluOpType as A, ActivationFunctionType as F
 
 NR = 4
 K = 128
-TW = 520
+G = 1
+R = 16 // G
+TW = 520 * G
 X4, U8, F32, BF, I32, U16, F16 = "float8_e4m3fn_x4", "uint8", "float32", "bfloat16", "int32", "uint16", "float16"
 
 SCRATCH = {
@@ -15,30 +17,32 @@ SCRATCH = {
     "qq": ("sbuf", [128, 512], X4), "pp": ("sbuf", [128, 512], U8),
     "psa": ("psum", [128, 2048], F32), "psb": ("psum", [128, 2048], F32),
     "pi": ("sbuf", [128, 32], I32),
-    "q16": ("sbuf", [128, 32], I32), "qof": ("sbuf", [128, 32], U16), "qf": ("sbuf", [128, 8], F32),
+    "q16": ("sbuf", [128, 40], I32), "qof": ("sbuf", [128, 32], U16), "qf": ("sbuf", [128, 8], F32),
     "i32": ("sbuf", [128, 32], BF), "e32": ("sbuf", [128, 32], BF),
     "b16": ("sbuf", [128, 16], BF), "m16": ("sbuf", [128, 16], BF), "mw": ("sbuf", [128, 512], BF),
     "mp": ("sbuf", [128, 256], BF), "blk": ("sbuf", [128, 8], F32), "mb": ("sbuf", [128, 8], F32),
     "gi": ("sbuf", [128, 64], F32), "gd": ("sbuf", [128, 64], BF),
     "dat": ("sbuf", [128, 128], BF), "num": ("sbuf", [128, 512], BF),
-    "sab": ("sbuf", [128, 512], F32), "scol": ("sbuf", [128, 4], F32), "k1": ("sbuf", [128, 512], F32),
-    "cmp": ("sbuf", [128, 1792], BF), "sg": ("sbuf", [128, 768], BF), "junk": ("sbuf", [128, 768], BF),
-    "cn": ("sbuf", [128, 4], F32), "scn": ("sbuf", [128, 1280], F16), "rof": ("sbuf", [128, 4], U16),
+    "sab": ("sbuf", [128, 512], F32), "scol": ("sbuf", [128, 4], F32), "offp": ("sbuf", [128, 128], BF),
+    "eqs": ("sbuf", [128, 512], BF), "tie": ("sbuf", [128, 512], BF),
+    "cmp": ("sbuf", [128, 2048], BF), "sg": ("sbuf", [128, 2048], BF), "junk": ("sbuf", [128, 2048], BF),
+    "cn": ("sbuf", [128, 4], F32), "scn": ("sbuf", [128, 1024], F16), "rof": ("sbuf", [128, 4], U16),
     "win": ("sbuf", [128, 512], BF), "win2": ("sbuf", [128, 8, 32], BF), "tr": ("sbuf", [128, 8, 32], BF),
-    "a0": ("sbuf", [128, 8], BF), "a1": ("sbuf", [128, 8], BF), "a2": ("sbuf", [128, 8], BF),
+    "a0": ("sbuf", [128, 8], BF), "a1": ("sbuf", [128, 8], BF),
     "ofs": ("sbuf", [128, 32], U16),
-    "ll": ("sbuf", [128, 32], U16), "xl": ("sbuf", [128, 8], U16),
-    "er32": ("sbuf", [128, 2048], F32), "dif": ("sbuf", [128, 512], F32),
-    "tab": ("sbuf", [128, 4, TW], F32), "pw": ("sbuf", [128, 512], BF), "pv": ("sbuf", [128, 384], BF),
-    "un": ("sbuf", [128, 896], F16), "c1": ("sbuf", [128, 48], F16), "c2": ("sbuf", [128, 48], F16),
-    "off": ("sbuf", [128, 56], U16), "gsum": ("sbuf", [128, 4, 128], F32), "accs": ("sbuf", [128, 2048], F32),
+    "la": ("sbuf", [128, 40], BF), "ll": ("sbuf", [128, 24], U16), "xl": ("sbuf", [128, 16], U16),
+    "xo": ("sbuf", [128, 2], U16),
+    "er32": ("sbuf", [128, 2048], F32), "dif": ("sbuf", [128, 512], F32), "dall": ("sbuf", [128, 2048], F32),
+    "tab": ("sbuf", [128, 4 // G, TW], F32), "pw": ("sbuf", [128, 512], BF), "pv": ("sbuf", [128, 384], BF),
+    "un": ("sbuf", [128, 896], F16), "c1": ("sbuf", [128, 48 * G], F16), "c2": ("sbuf", [128, 48 * G], F16),
+    "off": ("sbuf", [128, 56 * G], U16), "gsum": ("sbuf", [128, 4 // G, 128 * G], F32),
+    "accs": ("sbuf", [128, 512, 4], F32),
     "nbl": ("sbuf", [128, 128], F32), "scb": ("sbuf", [128, 128], F32),
 }
 
-EARLY = 1
-PIECES = (96, 160, 160, 96)
-GATHERS = (("s", 0, 0, 4), ("s", 1, 0, 2), ("s", 1, 2, 4), ("v", 2, 0, 1), ("v", 3, 0, 1), ("v", 2, 1, 2), ("v", 3, 1, 2),
-           ("s", 3, 2, 3), ("v", 2, 2, 3), ("s", 3, 3, 4), ("v", 2, 3, 4))
+PIECES = (64, 128, 160, 160)
+GATHERS = (("s", 0, 0, 2), ("s", 1, 0, 2), ("s", 0, 2, 4), ("v", 2, 0, 1), ("v", 3, 0, 1), ("v", 2, 1, 2), ("s", 3, 1, 2),
+           ("s", 1, 2, 4), ("v", 2, 2, 3), ("v", 3, 2, 3), ("s", 3, 3, 4), ("v", 2, 3, 4))
 
 SEMAPHORES = (["gp", "ve", "se", "te", "left", "ldu", "lde", "ster", "stnb", "stsc"]
               + ["ld%d" % i for i in range(4)] + ["sta%d" % i for i in range(len(PIECES))]
@@ -105,30 +109,37 @@ def rank_program(g, core, T, topo):
 
     ldu = dma("y", "ldu", T.u4[:, 0:4], T.u[:, 0:4])
     ld = {}
+
+    def load(q, a):
+        ld[a] = dma(q, "ld%d" % a, T.grt[:, 512 * a:512 * a + 512], T.gr[:, 512 * a:512 * a + 512])
+
     for a in range(4):
-        ld[a] = dma("s" if a % 2 == 0 else "y", "ld%d" % a, T.grt[:, 512 * a:512 * a + 512], T.gr[:, 512 * a:512 * a + 512])
+        load("sy"[a % 2], a)
 
     k_pi = did("g", g.iota(T.pi[:, :], [[0, 32]], 0, 1))
     k_ones = did("v", V.memset(T.ones[:, :], 1.0))
     k_ew0 = did("v", V.memset(T.ew[:, :], 0.0))
-    k_i32 = did("g", g.iota(T.i32[:, :], [[0, 2], [1, 16]], 0, 0, allow_small_or_imprecise_dtypes=True))
+    k_i32 = did("g", g.iota(T.i32[:, :], [[0, 32 // R], [1, R]], 0, 0, allow_small_or_imprecise_dtypes=True))
     need("g", k_ew0, k_ones)
     k_ew = did("g", g.affine_select(T.ew[:, 4:516:4], T.ones[:, 0:128], [[1, 128]], A.is_equal, 0.0, 0, -1))
     k_gi = did("g", g.iota(T.gi[:, :], [[128, 4], [1, 16]], -256, 1, allow_small_or_imprecise_dtypes=True))
+    k_off_p = did("g", g.affine_select(T.offp[:, :], T.ones[:, :], [[-1, 128]], A.not_equal, 0.0, 0, 1))
     g.dma_start(T.er32[:, :], T.gr[:, :]).then_inc(T.sem.lde, 16)
     k_er = ("lde", 16)
+    k_num = did("g", g.iota(T.num[:, :], [[1, 512]], -256, 0, allow_small_or_imprecise_dtypes=True))
 
+    did("v", V.memset(T.la[:, 32:40], 0.0))
     need("v", k_pi)
-    k = did("v", V.tensor_scalar(T.q16[:, :], T.pi[:, :], 15, None, A.bitwise_and))
+    k = did("v", V.tensor_scalar(T.q16[:, 0:32], T.pi[:, :], 15, None, A.bitwise_and))
     need("v", k)
     k_qf = did("v", V.tensor_copy(T.qf[:, 0:1], T.q16[:, 0:1]))
-    k_qof = did("v", V.tensor_copy(T.qof[:, :], T.q16[:, :]))
+    k_qof = did("v", V.tensor_copy(T.qof[:, :], T.q16[:, 0:32]))
     need("s", k_ones)
     for s in range(NR):
         k_blk = did("s", S.activation(T.blk[32 * s:32 * s + 32, 0:1], T.ones[32 * s:32 * s + 32, 0:1], F.Copy,
                                       scale=128.0 * place[s]))
     k_win = did("s", S.activation(T.win[:, 0:128], T.ones[:, :], F.Copy, scale=0.0))
-    k_tab = did("s", S.activation(T.tab[:, :, 0], T.ones[:, 0:4], F.Copy, scale=0.0))
+    k_tab = did("s", S.activation(T.tab[:, :, 0:G], T.ones[:, 0:4], F.Copy, scale=0.0))
     need("s", k_ew)
     k_pw = did("s", S.activation(T.pw[:, :], T.ew[:, 0:512], F.Copy, scale=0.0, bias=-256.0))
     need("v", k_i32, k_qf)
@@ -140,14 +151,11 @@ def rank_program(g, core, T, topo):
         c = slice(128 * b, 128 * b + 128)
         k_eq[b] = did("v", V.quantize_mx(T.eq[:, c], T.es[:, c], T.ew[:, 4 - b:516 - b]))
 
-    for b in range(EARLY):
-        unit(b)
-
     need("v", ldu)
     for t in range(4):
         k_u = did("v", V.tensor_scalar(T.urep[:, t:512:4], T.ones[:, :], T.u4[:, t:t + 1], None, A.mult))
 
-    k_gq, k_abs, k_scol, k_k1 = {}, {}, {}, {}
+    k_gq, k_abs, k_scol = {}, {}, {}
 
     def codes(a):
         need("v", ld[a])
@@ -164,44 +172,37 @@ def rank_program(g, core, T, topo):
         k_abs[a] = did("s", S.activation(T.sab[:, c], T.psa[:, o], F.Abs))
         need("s", k_col)
         k_scol[a] = did("s", S.activation(T.scol[:, a:a + 1], T.psb[:, 512 * a:512 * a + 1], F.Abs))
-        if a % 2:
-            need("g", k_abs[a])
-            c = slice(128 * a - 128, 128 * a + 128)
-            k_k1[a - 1] = k_k1[a] = did("g", g.affine_select(T.k1[:, c], T.sab[:, c], [[0, 2], [-1, 128]], A.is_gt, -1.0,
-                                                             0, 1))
 
-    at = [64 * a * (a + 3) for a in range(4)]
-    up = [0, 384, 640]
-
-    def below(a):
-        need("v", k_scol[a])
-        if a:
-            did("v", V.tensor_scalar(T.cmp[:, at[a]:at[a] + 128 * a], T.sab[:, 0:128 * a], T.scol[:, a:a + 1], None, A.is_ge))
-        o = at[a] + 128 * a
-        did("v", V.tensor_scalar(T.cmp[:, o:o + 128], T.sab[:, 128 * a:128 * a + 128], T.scol[:, a:a + 1], None, A.is_gt))
-
-    def ties(a):
-        need("v", k_k1[a])
-        o = at[a] + 128 * a + 128
-        return did("v", V.tensor_scalar(T.cmp[:, o:o + 128], T.k1[:, 128 * a:128 * a + 128], T.scol[:, a:a + 1], None,
-                                        A.is_equal))
+    def compare(a, lo, hi, op):
+        need("v", k_scol[a], k_abs[hi - 1])
+        return did("v", V.tensor_scalar(T.cmp[:, 512 * a + 128 * lo:512 * a + 128 * hi], T.sab[:, 128 * lo:128 * hi],
+                                        T.scol[:, a:a + 1], None, op))
 
     def signs(a, lo, hi):
-        o = up[a] + lo - 128 * (a + 1)
-        need("s", k_scol[a], k_abs[hi // 128 - 1])
-        return did("s", S.activation(T.sg[:, o:o + hi - lo], T.sab[:, lo:hi], F.Sign, bias=T.scol[:, a:a + 1], scale=-1.0))
+        need("s", k_scol[a], k_abs[hi - 1])
+        return did("s", S.activation(T.sg[:, 512 * a + 128 * lo:512 * a + 128 * hi], T.sab[:, 128 * lo:128 * hi], F.Sign,
+                                     bias=T.scol[:, a:a + 1], scale=-1.0))
 
-    def above(a, k):
-        c = slice(up[a], up[a] + 384 - 128 * a)
+    def tally(a, lo, hi, scale, k):
+        c = slice(512 * a + 128 * lo, 512 * a + 128 * hi)
         need("s", k)
-        return did("s", S.activation(T.junk[:, c], T.sg[:, c], F.Relu, scale=-1.0, accum_out=T.cn[:, a:a + 1]))
+        return did("s", S.activation(T.junk[:, c], T.sg[:, c], F.Relu, scale=scale, accum_out=T.cn[:, a:a + 1]))
 
-    def add_up(a, *toks):
-        n = 64 * a + 128
+    def equal(a):
+        c = slice(128 * a, 128 * a + 128)
+        need("v", k_scol[a])
+        return did("v", V.tensor_scalar(T.eqs[:, c], T.sab[:, c], T.scol[:, a:a + 1], -1.0, A.is_equal, A.mult))
+
+    def ties(a, k):
+        c = slice(128 * a, 128 * a + 128)
+        need("v", k, k_off_p)
+        return did("v", V.tensor_tensor_scan(T.tie[:, c], T.offp[:, :], T.eqs[:, c], 0.0, A.mult, A.add))
+
+    def add_up(a, lo, hi, *toks):
+        n, o = 64 * (hi - lo), 512 * a + 128 * lo
         need("v", *toks)
-        return did("v", V.tensor_tensor_scan(T.scn[:, 320 * a + 320 - n:320 * a + 320], T.cmp[:, at[a]:at[a] + n],
-                                             T.cmp[:, at[a] + n:at[a] + 2 * n], T.cn[:, a:a + 1] if a < 3 else 0.0,
-                                             A.add, A.add))
+        return did("v", V.tensor_tensor_scan(T.scn[:, 256 * a + 256 - n:256 * a + 256], T.cmp[:, o:o + n],
+                                             T.cmp[:, o + n:o + 2 * n], T.tie[:, 128 * a + 127:128 * a + 128], A.add, A.add))
 
     codes(0)
     need("v", k_u)
@@ -210,93 +211,98 @@ def rank_program(g, core, T, topo):
         codes(a)
     for a in range(4):
         score(a)
-    k_b16 = did("v", V.tensor_scalar(T.b16[:, :], T.e32[:, 1:17], -2.0, None, A.mult))
-    need("v", k_blk, k_gi)
+    unit(0)
+    unit(1)
+    need("v", k_gi)
     k_gd = did("v", V.tensor_scalar(T.gd[:, :], T.gi[:, :], T.qf[:, 0:1], None, A.subtract))
-    for i in (2, 3):
-        k_mb = did("v", V.tensor_scalar(T.mb[:, i:i + 1], T.blk[:, 0:1], 128.0 * i, -4096.0, A.is_ge, A.mult))
-    need("v", k_b16)
-    k_m16 = did("v", V.tensor_tensor(T.m16[:, :], T.e32[:, 0:16], T.b16[:, :], A.add))
+    signs(0, 1, 3)
+    k_sg = {0: signs(0, 3, 4), 1: signs(1, 2, 4)}
+    k_up = {0: tally(0, 1, 4, -1.0, k_sg[0])}
+    k_sg.update({2: signs(2, 3, 4), 3: signs(3, 0, 1)})
+    k_up.update({1: tally(1, 2, 4, -1.0, k_sg[1]), 2: tally(2, 3, 4, -1.0, k_sg[2]), 3: tally(3, 0, 1, 1.0, k_sg[3])})
+    span = {0: (0, 1), 1: (0, 2), 2: (0, 3), 3: (1, 4)}
+    k_ge, k_same, k_tie = {}, {}, {}
+    for a in (0, 1):
+        k_ge[a], k_same[a] = compare(a, *span[a], A.is_ge), equal(a)
+    for a in (0, 1):
+        k_same[a + 2] = equal(a + 2)
+        k_tie[a] = ties(a, k_same[a])
+    k_ge[2] = compare(2, *span[2], A.is_ge)
+    k_tie.update({2: ties(2, k_same[2]), 3: ties(3, k_same[3])})
+    k_ge[3] = compare(3, *span[3], A.is_ge)
+    k_sum = {a: add_up(a, *span[a], k_ge[a], k_tie[a]) for a in range(4)}
     for a in range(4):
-        below(a)
-    signs(0, 128, 384)
-    k_sg = {0: signs(0, 384, 512), 1: signs(1, 256, 512)}
-    k_up = {0: above(0, k_sg[0])}
-    k_sg[2] = signs(2, 384, 512)
-    for a in (1, 2):
-        k_up[a] = above(a, k_sg[a])
-    k_tie = {a: ties(a) for a in (0, 1)}
-    add_up(0, k_tie[0], k_up[0])
-    for a in (3, 2):
-        k_tie[a] = ties(a)
-    k_num = did("g", g.iota(T.num[:, :], [[1, 512]], -256, 0, allow_small_or_imprecise_dtypes=True))
-    add_up(1, k_tie[1], k_up[1])
-    add_up(3, k_tie[3])
-    k = add_up(2, k_tie[2], k_up[2])
-    spare = list(range(EARLY, 4))
+        need("v", k_sum[a], k_up[a])
+        last = (T.rof[:, a:a + 1], T.scn[:, 256 * a + 255:256 * a + 256], T.cn[:, a:a + 1])
+        k_r = did("v", V.tensor_scalar(*last, None, A.add) if a < 3 else V.tensor_scalar(*last, 128.0, A.subtract, A.add))
 
-    def then(*toks):
-        if spare:
-            unit(spare.pop())
-        need("v", *toks)
-
-    then(k)
-    k_r = did("v", V.tensor_copy(T.rof[:, :], T.scn[:, 319:1280:320]))
-
-    then(k_r, k_win, k_gd)
+    unit(2)
+    need("v", k_r, k_win, k_gd)
     k_w = did("v", V.tensor_copy(T.win[:, 0:512].indirect(T.rof[:, 0:4]), T.gd[:, :]))
-    then(k_w)
+    unit(3)
+    need("v", k_w, k_blk)
     did("v", V.tensor_copy(T.win2[:, :, 0:16], T.win[:, 0:128]))
     d2 = did("v", V.tensor_copy(T.win2[:, :, 16:32], T.win[:, 0:128]))
+    did("v", V.tensor_scalar(T.b16[:, :], T.e32[:, 1:17], -2.0, None, A.mult))
+    k_xo = did("v", V.tensor_scalar(T.xo[:, 0:1], T.blk[:, 0:1], 1.0 / 16, T.qf[:, 0:1], A.mult, A.add))
     need("v", d2)
     k_tr = did("v", V.transpose(T.tr[:, :, :], T.win2[:, :, :]))
+    for i in (2, 3):
+        k_mb = did("v", V.tensor_scalar(T.mb[:, i:i + 1], T.blk[:, 0:1], 128.0 * i, -4096.0, A.is_ge, A.mult))
     need("v", k_tr)
     k_a0 = did("v", V.tensor_tensor(T.a0[:, :], T.tr[:, :, 0], T.tr[:, :, 16], A.add))
+    k_m16 = did("v", V.tensor_tensor(T.m16[:, :], T.e32[:, 0:16], T.b16[:, :], A.add))
+    did("v", V.tensor_scalar(T.qf[:, 4:5], T.b16[:, 15:16], -1.0, -256.0, A.mult, A.add))
     need("v", k_a0)
     k_a1 = did("v", V.tensor_tensor(T.a1[0:64, :], T.a0[0:64, :], T.a0[64:128, :], A.add))
     need("v", k_a1)
+    c = slice(8 * place[me], 8 * place[me] + 8)
     for b in range(4):
-        k_a2 = did("v", V.tensor_tensor(T.a2[32 * b:32 * b + 32, :], T.a1[0:32, :], T.a1[32:64, :], A.add))
-
-    def listed(i):
-        return T.ll[:, 8 * i:8 * i + 8]
-
-    need("v", k_a2)
-    k_lst = did("v", V.tensor_scalar(listed(place[me]), T.a2[:, :], 256.0, None, A.add))
+        k_lst = did("v", V.tensor_tensor(T.la[32 * b:32 * b + 32, c], T.a1[0:32, :], T.a1[32:64, :], A.add))
+    need("v", k_lst)
     k_of = {}
-    for t in (2, 3, 0, 1):
-        k_of[t] = did("v", V.tensor_scalar(T.ofs[:, 8 * t:8 * t + 8], T.a2[:, :], 4.0, 1024.0 + t, A.mult, A.add))
+    for t in (2, 0, 3, 1):
+        k_of[t] = did("v", V.tensor_scalar(T.ofs[:, 8 * t:8 * t + 8], T.la[:, c], 4.0, 1024.0 + t, A.mult, A.add))
     k_sel = {}
     for t in (0, 1):
         need("v", k_of[t])
         k_sel[t] = did("v", V.tensor_copy(T.sel[:, t:512:4], T.grt[:, 0:2048].indirect(T.ofs[:, 8 * t:8 * t + 8])))
-    need("s", k_m16, k_qof)
+    k_sel[3] = did("v", V.tensor_copy(T.sel[:, 259:512:4], T.grt[:, 0:2048].indirect(T.ofs[:, 28:32])))
+    for b in range(4):
+        need("t", k_abs[3], k_eq[b])
+        k = did("t", TE.matmul_mx(T.psa[:, 512 * b:512 * b + 512], T.eq[:, 128 * b:128 * b + 128],
+                                  T.es[:, 128 * b:128 * b + 128], T.gq[:, :], T.gs[:, :], True, True))
+        need("s", k)
+        k_all = did("s", S.activation(T.dall[:, b:2048:4], T.psa[:, 512 * b:512 * b + 512], F.Copy, scale=-1.0))
+    need("s", k_of[2])
+    did("s", S.activation(T.sel[:, 2:512:4], T.grt[:, 0:2048].indirect(T.ofs[:, 16:24]), F.Copy))
+    need("s", k_of[3])
+    k_sel[2] = did("s", S.activation(T.sel[:, 3:256:4], T.grt[:, 0:2048].indirect(T.ofs[:, 24:28]), F.Copy))
+    need("s", k_m16, k_qof, k_mb, k_num)
     k_mw = did("s", S.activation(T.mw[:, :], T.m16[:, 0:16].indirect(T.qof[:, :]), F.Copy))
-    for t in (2, 3):
-        need("s", k_of[t])
-        k_sel[t] = did("s", S.activation(T.sel[:, t:512:4], T.grt[:, 0:2048].indirect(T.ofs[:, 8 * t:8 * t + 8]), F.Copy))
-    need("s", k_mw, k_mb, k_num)
     k_dat = did("s", S.activation(T.dat[:, :], T.num[:, 1:129], F.Identity, bias=T.blk[:, 0:1]))
+    need("s", k_mw)
     for i in (2, 3):
         k_mp = did("s", S.activation(T.mp[:, 128 * i - 256:128 * i - 128], T.mw[:, 0:128], F.Identity,
                                      bias=T.mb[:, i:i + 1]))
-    need("v", k_sel[1], k_sel[3])
+    need("v", *k_sel.values())
     k_q = did("v", V.quantize_mx(T.qq[:, 0:128], T.pp[:, 0:128], T.sel[:, :]))
 
     sent = [0]
 
-    def send(src, dst, sem):
+    def send(src, dst, sem, step=1):
         tr = []
         for c in plan:
             rid, pid, _ = topo.addr(c)
             slots, theirs = view_of(T.rank_of(c), T.cores, topo)
-            tr.append(RemoteDMATransfer(dst_ids=[DstId(rid=rid, pnc=pid)], dma_engine_mask=sum(1 << e for e in plan[c]),
+            use = plan[c][::step]
+            tr.append(RemoteDMATransfer(dst_ids=[DstId(rid=rid, pnc=pid)], dma_engine_mask=sum(1 << e for e in use),
                                         remote_sem=T.sem[sem], src=src, dst=dst(128 * slots.index(me), theirs.index(me))))
-            sent[0] += len(plan[c])
+            sent[0] += len(use)
         g.remote_dma_fused(tr, local_sem=T.sem.left)
 
     need("g", k_lst)
-    send(listed(place[me]), lambda c, i: listed(i), "al%d" % me)
+    send(T.la[:, c], lambda c, i: T.la[:, 8 * i:8 * i + 8], "al%d" % me)
     need("g", k_q)
     send(T.qq[:, 0:128].bitcast(dt.uint8), lambda c, i: T.qq[:, c:c + 128].bitcast(dt.uint8), "ac%d" % me)
     send(T.pp[:, 0:128], lambda c, i: T.pp[:, c:c + 128], "ac%d" % me)
@@ -304,14 +310,14 @@ def rank_program(g, core, T, topo):
     heard = {s: ("al%d" % s, narr[s]) for s in narr}
     heard[me] = k_lst
 
-    def decode(bank, lo, hi, *toks):
-        need("t", *k_eq.values(), *toks)
-        return [did("t", TE.matmul_mx(bank[:, 512 * b:512 * b + hi - lo], T.eq[:, 128 * b:128 * b + 128],
-                                      T.es[:, 128 * b:128 * b + 128], T.qq[:, lo:hi], T.pp[:, lo:hi], True, True))
-                for b in range(4)]
+    def decode(bank, lo, hi, *toks, rows=range(4)):
+        need("t", *toks)
+        return {b: did("t", TE.matmul_mx(bank[:, 512 * b:512 * b + hi - lo], T.eq[:, 128 * b:128 * b + 128],
+                                         T.es[:, 128 * b:128 * b + 128], T.qq[:, lo:hi], T.pp[:, lo:hi], True, True))
+                for b in rows}
 
     def region(i, b):
-        return T.tab[:, b, 1 + 128 * i:129 + 128 * i]
+        return T.tab[:, b // G, G * (1 + 128 * i) + b % G:G * (129 + 128 * i):G]
 
     kept = {}
 
@@ -320,28 +326,23 @@ def rank_program(g, core, T, topo):
             need("s", dec[b])
             kept[place[s], b] = did("s", S.activation(region(place[s], b), bank[:, 512 * b:512 * b + 128], F.Copy))
 
-    def block(s):
-        need("v", heard[s])
-        return did("v", V.tensor_copy(T.xl[32 * s:32 * s + 32, :], T.ll[32 * s:32 * s + 32, 8 * place[s]:8 * place[s] + 8]))
-
-    dec = decode(T.psa, 0, 128, k_q, k_abs[3])
+    dec = decode(T.psa, 0, 128, k_q, k_all)
     need("t", k_scol[3])
     k_sc = did("t", TE.matmul_mx(T.psb[:, 0:128], T.uq[:, :], T.us[:, :], T.qq[:, 0:128], T.pp[:, 0:128], True, True))
-    block(me)
     k_dif = {}
+    need("v", k_all)
     for b in range(4):
-        need("v", dec[b])
-        k_dif[b] = did("v", V.tensor_tensor(T.dif[:, 128 * b:128 * b + 128], T.sel[:, b:512:4],
-                                            T.psa[:, 512 * b:512 * b + 128], A.subtract))
+        k_dif[b] = did("v", V.tensor_tensor(T.dif[:, 128 * b:128 * b + 128],
+                                            T.dall[:, 0:2048].indirect(T.ofs[:, 8 * b:8 * b + 8]), T.sel[:, b:512:4], A.add))
     k_ers = [k_er]
 
-    def place_er(b):
-        need("v", k_dif[b], *k_ers)
-        k_ers[:] = [did("v", V.tensor_copy(T.er32[:, 0:2048].indirect(T.ofs[:, 8 * b:8 * b + 8]),
-                                           T.dif[:, 128 * b:128 * b + 128]))]
+    def place_er(lo, hi):
+        need("v", k_dif[hi - 1], *k_ers)
+        k_ers[:] = [did("v", V.tensor_copy(T.er32[:, 0:2048].indirect(T.ofs[:, 8 * lo:8 * hi]),
+                                           T.dif[:, 128 * lo:128 * hi]))]
 
-    place_er(0)
-    keep(me, T.psa, k_dif)
+    place_er(0, 1)
+    keep(me, T.psa, dec)
     need("s", k_sc)
     k_scb = did("s", S.activation(T.scb[:, :], T.psb[:, 0:128], F.Abs))
 
@@ -352,35 +353,38 @@ def rank_program(g, core, T, topo):
     def copy(q, out, src):
         return did(q, S.activation(out, src, F.Copy) if q == "s" else V.tensor_copy(out, src))
 
-    def window(i, b):
-        return T.tab[:, b, 0:1 + 128 * i].indirect(T.off[:, 8 * i - 8:8 * i])
+    def window(i, h):
+        return T.tab[:, h, 0:G * (1 + 128 * i)].indirect(T.off[:, 8 * G * (i - 1):8 * G * i])
 
-    for s in (mate, x, y):
-        k_xl = block(s)
-    place_er(1)
+    def offsets(out, src, rows):
+        return did("v", V.tensor_scalar(out, src, 1.0 * G, T.qf[rows, 4:5], A.mult, A.add))
+
+    need("v", k_xo, *heard.values())
+    k_xl = did("v", V.tensor_scalar(T.xl[:, :], T.la[:, 0:40].indirect(T.xo[:, 0:1]), 256.0, None, A.add))
+    did("v", V.tensor_scalar(T.ll[:, :], T.la[:, 8:32], 256.0, None, A.add))
+    place_er(1, 2)
     need("v", k_xl, k_pw, k_dat)
-    k_en = did("v", V.tensor_copy(T.pw[:, 0:512].indirect(T.xl[:, :]), T.dat[:, :]))
-    place_er(2)
+    k_en = did("v", V.tensor_copy(T.pw[:, 0:512].indirect(T.xl[:, 0:8]), T.dat[:, :]))
+    place_er(2, 3)
     need("s", k_xl)
-    k_nb = did("s", S.activation(T.nbl[:, :], T.num[:, 0:512].indirect(T.xl[:, :]), F.Copy, bias=256.0))
-    need("s", k_en, *heard.values())
-    k_pv = did("s", S.activation(T.pv[:, 128:384], T.pw[:, 0:512].indirect(T.ll[:, 16:32]), F.Copy))
+    k_nb = did("s", S.activation(T.nbl[:, :], T.num[:, 0:512].indirect(T.xl[:, 0:8]), F.Copy, bias=256.0))
+    need("s", k_en)
+    k_pv = did("s", S.activation(T.pv[:, 128:384], T.pw[:, 0:512].indirect(T.ll[:, 8:24]), F.Copy))
     need("v", k_en)
-    k = did("v", V.tensor_copy(T.pv[:, 0:128], T.pw[:, 0:512].indirect(listed(1))))
+    k = did("v", V.tensor_copy(T.pv[:, 0:128], T.pw[:, 0:512].indirect(T.ll[:, 0:8])))
     unfold(T.un[:, 384:896], T.pw[:, :], T.mw[:, :], k_mw)
     k = unfold(T.un[:, 0:128], T.pv[:, 0:128], T.mw[:, 0:128], k)
-    place_er(3)
+    place_er(3, 4)
     need("v", k)
     first = slice(32 * order[0], 32 * order[0] + 32)
     for h in range(0, 128, 32):
-        k_off1 = did("v", V.tensor_scalar(T.off[h:h + 32, 0:8], T.un[first, 15:128:16], T.b16[first, 15:16], -256.0,
-                                          A.subtract, A.add))
+        k_off1 = offsets(T.off[h:h + 32, 0:8 * G], T.un[first, R - 1:128:R], first)
     k = unfold(T.un[:, 128:384], T.pv[:, 128:384], T.mp[:, :], k_pv, k_mp)
     need("y", k_scb)
     ends = [dma("y", "stsc", T.sc[:, :], T.scb[0:1, :])]
     need("y", k_nb)
     ends.append(dma("y", "stnb", T.nb[:, :], T.nbl[0:128:32, :]))
-    need("y", *k_ers)
+    need("y", ("left", sent[0]), *k_ers)
     ends.append(dma("y", "ster", T.er[:, :], T.er32[:, :]))
 
     mine = list(kept.values())
@@ -388,51 +392,55 @@ def rank_program(g, core, T, topo):
     theirs = list(kept.values())
     fetched, summed = {}, {}
 
-    def fetch(q, b):
-        need(q, k_off1, k_tab, kept[0, b])
-        fetched[b] = copy(q, T.gsum[:, b, :], window(1, b))
+    def fetch(q, h):
+        need(q, k_off1, k_tab, kept[0, G * h + G - 1])
+        fetched[h] = copy(q, T.gsum[:, h, :], window(1, h))
 
     def add(b):
-        need("v", fetched[b], dx[b])
-        summed[b] = did("v", V.tensor_tensor(region(1, b), T.gsum[:, b, :], T.psa[:, 512 * b:512 * b + 128], A.add))
+        need("v", fetched[b // G], dx[b])
+        summed[b // G] = did("v", V.tensor_tensor(region(1, b), T.gsum[:, b // G, b % G:128 * G:G],
+                                                  T.psa[:, 512 * b:512 * b + 128], A.add))
 
-    for b in (1, 2, 3):
-        fetch("s", b)
-    dx = decode(T.psa, 256, 384, got[x], *mine)
-    keep(y, T.psb, decode(T.psb, 384, 512, got[y], *theirs))
+    for h in range(1, 4 // G):
+        fetch("s", h)
+    dx, dy = {}, {}
+    for rows in ((0, 1), (2, 3)):
+        dx.update(decode(T.psa, 256, 384, got[x], *mine, rows=rows))
+        dy.update(decode(T.psb, 384, 512, got[y], *theirs, rows=rows))
+    keep(y, T.psb, dy)
     fetch("v", 0)
     need("v", k)
-    k = did("v", V.tensor_tensor(T.c1[0:64, :], T.un[0:64, 143:896:16], T.un[64:128, 143:896:16], A.max))
-    add(0)
+    k = did("v", V.tensor_tensor(T.c1[0:64, :], T.un[0:64, 127 + R:896:R], T.un[64:128, 127 + R:896:R], A.max))
     need("v", k)
     for h in (0, 32):
         k = did("v", V.tensor_tensor(T.c2[h:h + 32, :], T.c1[0:32, :], T.c1[32:64, :], A.max))
+    add(0)
     add(1)
     need("v", k)
     for h in (0, 64):
-        k_off = did("v", V.tensor_scalar(T.off[h:h + 64, 8:56], T.c2[0:64, :], T.b16[0:64, 15:16], -256.0, A.subtract,
-                                         A.add))
+        k_off = offsets(T.off[h:h + 64, 8 * G:56 * G], T.c2[0:64, :], slice(0, 64))
     add(2)
     add(3)
 
     for pair in ((0, 1), (2, 3)):
-        for i in (2, 3):
-            for b in pair:
-                need("v", k_off, kept[i, b], summed[b])
-                summed[b] = did("v", V.tensor_tensor(region(i, b), window(i, b), region(i, b), A.add))
+        for i, h in [(i, h) for i in (2, 3) for h in pair]:
+            need("v", k_off, kept[i, G * h + G - 1], summed[h])
+            o = T.tab[:, h, G * (1 + 128 * i):G * (129 + 128 * i)]
+            summed[h] = did("v", V.tensor_tensor(o, window(i, h), o, A.add))
 
     edges = [sum(PIECES[:i]) for i in range(len(PIECES) + 1)]
     done = {i: [] for i in range(len(PIECES))}
-    for q, b, i, j in GATHERS:
+    for q, h, i, j in GATHERS:
         lo, hi = edges[i], edges[j]
-        need(q, summed[b])
-        k = copy(q, T.accs[:, 4 * lo + b:4 * hi:4], T.tab[:, b, 0:513].indirect(T.off[:, 24 + lo // 16:24 + hi // 16]))
+        need(q, summed[h])
+        k = copy(q, T.accs[:, lo:hi, h],
+                 T.tab[:, h, 0:513 * G].indirect(T.off[:, 24 * G + lo // R:24 * G + hi // R]))
         for n in range(i, j):
             done[n].append(k)
     for i in done:
         need("y", *done[i])
-        c = slice(4 * edges[i], 4 * edges[i + 1])
-        ends.append(dma("y", "sta%d" % i, T.acc[:, c], T.accs[:, c]))
+        lo, hi = edges[i], edges[i + 1]
+        ends.append(dma("y", "sta%d" % i, T.acc[:, 4 * lo:4 * hi], T.accs[:, lo:hi, :]))
 
     need("y", *ends)
     need("g", ("left", sent[0]), *[(sem, count[sem]) for sem in ("gp", "ve", "se", "te")])

from concourse.bass import DstId, RemoteDMATransfer
from concourse.mybir import dt, AluOpType as A, ActivationFunctionType as F

NR = 4
K = 128
G = 1
R = 16 // G
TW = 520 * G
X4, U8, F32, BF, I32, U16, F16 = "float8_e4m3fn_x4", "uint8", "float32", "bfloat16", "int32", "uint16", "float16"

SCRATCH = {
    "u4": ("sbuf", [128, 16], BF), "grt": ("sbuf", [128, 2048], BF), "urep": ("sbuf", [128, 512], BF),
    "sel": ("sbuf", [128, 512], BF), "ones": ("sbuf", [128, 128], BF), "ew": ("sbuf", [128, 520], BF),
    "uq": ("sbuf", [128, 128], X4), "us": ("sbuf", [128, 128], U8),
    "gq": ("sbuf", [128, 512], X4), "gs": ("sbuf", [128, 512], U8),
    "eq": ("sbuf", [128, 512], X4), "es": ("sbuf", [128, 512], U8),
    "qq": ("sbuf", [128, 512], X4), "pp": ("sbuf", [128, 512], U8),
    "psa": ("psum", [128, 2048], F32), "psb": ("psum", [128, 2048], F32),
    "pi": ("sbuf", [128, 32], I32),
    "q16": ("sbuf", [128, 40], I32), "qof": ("sbuf", [128, 32], U16), "qf": ("sbuf", [128, 8], F32),
    "i32": ("sbuf", [128, 32], BF), "e32": ("sbuf", [128, 32], BF),
    "b16": ("sbuf", [128, 16], BF), "m16": ("sbuf", [128, 16], BF), "mw": ("sbuf", [128, 512], BF),
    "mp": ("sbuf", [128, 256], BF), "blk": ("sbuf", [128, 8], F32), "mb": ("sbuf", [128, 8], F32),
    "gi": ("sbuf", [128, 64], F32), "gd": ("sbuf", [128, 64], BF),
    "dat": ("sbuf", [128, 128], BF), "num": ("sbuf", [128, 512], BF),
    "sab": ("sbuf", [128, 512], F32), "scol": ("sbuf", [128, 4], F32), "offp": ("sbuf", [128, 128], BF),
    "eqs": ("sbuf", [128, 512], BF), "tie": ("sbuf", [128, 512], BF),
    "cmp": ("sbuf", [128, 2048], BF), "sg": ("sbuf", [128, 2048], BF), "junk": ("sbuf", [128, 2048], BF),
    "cn": ("sbuf", [128, 4], F32), "scn": ("sbuf", [128, 1024], F16), "rof": ("sbuf", [128, 4], U16),
    "win": ("sbuf", [128, 512], BF), "win2": ("sbuf", [128, 8, 32], BF), "tr": ("sbuf", [128, 8, 32], BF),
    "a0": ("sbuf", [128, 8], BF), "a1": ("sbuf", [128, 8], BF),
    "ofs": ("sbuf", [128, 32], U16),
    "la": ("sbuf", [128, 40], BF), "ll": ("sbuf", [128, 24], U16), "xl": ("sbuf", [128, 16], U16),
    "xo": ("sbuf", [128, 2], U16),
    "er32": ("sbuf", [128, 2048], F32), "dif": ("sbuf", [128, 512], F32), "dall": ("sbuf", [128, 2048], F32),
    "tab": ("sbuf", [128, 4 // G, TW], F32), "pw": ("sbuf", [128, 512], BF), "pv": ("sbuf", [128, 384], BF),
    "un": ("sbuf", [128, 896], F16), "c1": ("sbuf", [128, 48 * G], F16), "c2": ("sbuf", [128, 48 * G], F16),
    "off": ("sbuf", [128, 56 * G], U16), "gsum": ("sbuf", [128, 4 // G, 128 * G], F32),
    "accs": ("sbuf", [128, 512, 4], F32),
    "nbl": ("sbuf", [128, 128], F32), "scb": ("sbuf", [128, 128], F32),
}

PIECES = (64, 128, 160, 160)
GATHERS = (("s", 0, 0, 2), ("s", 1, 0, 2), ("s", 0, 2, 4), ("v", 2, 0, 1), ("v", 3, 0, 1), ("v", 2, 1, 2), ("s", 3, 1, 2),
           ("s", 1, 2, 4), ("v", 2, 2, 3), ("v", 3, 2, 3), ("s", 3, 3, 4), ("v", 2, 3, 4))

SEMAPHORES = (["gp", "ve", "se", "te", "left", "ldu", "lde", "ster", "stnb", "stsc"]
              + ["ld%d" % i for i in range(4)] + ["sta%d" % i for i in range(len(PIECES))]
              + ["al%d" % i for i in range(NR)] + ["ac%d" % i for i in range(NR)])


def engines_of(src, cores, topo):
    dsts = [c for c in cores if c != src]
    off = [c for c in dsts if topo.chip(c) != topo.chip(src)]
    on = [c for c in dsts if c not in off]
    plan, used = {}, []
    for i, c in enumerate(off):
        e = topo.engines(src, c)
        n = len(e) // len(off)
        plan[c] = e[i * n:(i + 1) * n]
        used += plan[c]
    width = len(used) // len(off)
    for c in on:
        plan[c] = [x for x in topo.engines(src, c) if x not in used][:width]
        used += plan[c]
    return plan


def view_of(r, cores, topo):
    near = [s for s in range(NR) if s != r and topo.chip(cores[s]) == topo.chip(cores[r])]
    far = [s for s in range(NR) if s != r and s not in near]
    return [r] + near + far, ([0, 1, 2, 3] if far[0] else [1, 0, 2, 3])


def rank_program(g, core, T, topo):
    rank = T.rank_of(core)
    if rank is None:
        return
    queues = {"g": g, "v": g.vector, "s": g.scalar, "t": g.tensor, "y": g.sync}
    count = {"gp": 0, "ve": 0, "se": 0, "te": 0}
    own = {"g": "gp", "v": "ve", "s": "se", "t": "te"}
    seen = {}

    def need(q, *toks):
        best = {}
        for tk in toks:
            best[tk[0]] = max(best.get(tk[0], 0), tk[1])
        for sem in best:
            if seen.get((q, sem), 0) < best[sem]:
                queues[q].wait_ge(T.sem[sem], best[sem])
                seen[(q, sem)] = best[sem]

    def did(q, ins):
        sem = own[q]
        ins.then_inc(T.sem[sem], 1)
        count[sem] += 1
        return (sem, count[sem])

    def dma(q, sem, out, in_):
        queues[q].dma_start(out, in_).then_inc(T.sem[sem], 16)
        return (sem, 16)

    V, S, TE = g.vector, g.scalar, g.tensor
    me = rank
    (_, mate, x, y), order = view_of(me, T.cores, topo)
    place = {s: i for i, s in enumerate(order)}
    plan = engines_of(core, T.cores, topo)
    narr = {s: len(engines_of(T.cores[s], T.cores, topo)[core]) for s in range(NR) if s != me}

    ldu = dma("y", "ldu", T.u4[:, 0:4], T.u[:, 0:4])
    ld = {}

    def load(q, a):
        ld[a] = dma(q, "ld%d" % a, T.grt[:, 512 * a:512 * a + 512], T.gr[:, 512 * a:512 * a + 512])

    for a in range(4):
        load("sy"[a % 2], a)

    k_pi = did("g", g.iota(T.pi[:, :], [[0, 32]], 0, 1))
    k_ones = did("v", V.memset(T.ones[:, :], 1.0))
    k_ew0 = did("v", V.memset(T.ew[:, :], 0.0))
    k_i32 = did("g", g.iota(T.i32[:, :], [[0, 32 // R], [1, R]], 0, 0, allow_small_or_imprecise_dtypes=True))
    need("g", k_ew0, k_ones)
    k_ew = did("g", g.affine_select(T.ew[:, 4:516:4], T.ones[:, 0:128], [[1, 128]], A.is_equal, 0.0, 0, -1))
    k_gi = did("g", g.iota(T.gi[:, :], [[128, 4], [1, 16]], -256, 1, allow_small_or_imprecise_dtypes=True))
    k_off_p = did("g", g.affine_select(T.offp[:, :], T.ones[:, :], [[-1, 128]], A.not_equal, 0.0, 0, 1))
    g.dma_start(T.er32[:, :], T.gr[:, :]).then_inc(T.sem.lde, 16)
    k_er = ("lde", 16)
    k_num = did("g", g.iota(T.num[:, :], [[1, 512]], -256, 0, allow_small_or_imprecise_dtypes=True))

    did("v", V.memset(T.la[:, 32:40], 0.0))
    need("v", k_pi)
    k = did("v", V.tensor_scalar(T.q16[:, 0:32], T.pi[:, :], 15, None, A.bitwise_and))
    need("v", k)
    k_qf = did("v", V.tensor_copy(T.qf[:, 0:1], T.q16[:, 0:1]))
    k_qof = did("v", V.tensor_copy(T.qof[:, :], T.q16[:, 0:32]))
    need("s", k_ones)
    for s in range(NR):
        k_blk = did("s", S.activation(T.blk[32 * s:32 * s + 32, 0:1], T.ones[32 * s:32 * s + 32, 0:1], F.Copy,
                                      scale=128.0 * place[s]))
    k_win = did("s", S.activation(T.win[:, 0:128], T.ones[:, :], F.Copy, scale=0.0))
    k_tab = did("s", S.activation(T.tab[:, :, 0:G], T.ones[:, 0:4], F.Copy, scale=0.0))
    need("s", k_ew)
    k_pw = did("s", S.activation(T.pw[:, :], T.ew[:, 0:512], F.Copy, scale=0.0, bias=-256.0))
    need("v", k_i32, k_qf)
    k_e32 = did("v", V.tensor_scalar(T.e32[:, :], T.i32[:, :], T.qf[:, 0:1], 512.0, A.is_equal, A.mult))
    k_eq = {}

    def unit(b):
        need("v", k_ew)
        c = slice(128 * b, 128 * b + 128)
        k_eq[b] = did("v", V.quantize_mx(T.eq[:, c], T.es[:, c], T.ew[:, 4 - b:516 - b]))

    need("v", ldu)
    for t in range(4):
        k_u = did("v", V.tensor_scalar(T.urep[:, t:512:4], T.ones[:, :], T.u4[:, t:t + 1], None, A.mult))

    k_gq, k_abs, k_scol = {}, {}, {}

    def codes(a):
        need("v", ld[a])
        c = slice(128 * a, 128 * a + 128)
        k_gq[a] = did("v", V.quantize_mx(T.gq[:, c], T.gs[:, c], T.grt[:, 512 * a:512 * a + 512]))

    def score(a):
        c = slice(128 * a, 128 * a + 128)
        need("t", k_uq, k_gq[a])
        o = slice(512 * a, 512 * a + 128)
        k_row = did("t", TE.matmul_mx(T.psa[:, o], T.uq[:, :], T.us[:, :], T.gq[:, c], T.gs[:, c], True, True))
        k_col = did("t", TE.matmul_mx(T.psb[:, o], T.gq[:, c], T.gs[:, c], T.uq[:, :], T.us[:, :], True, True))
        need("s", k_row)
        k_abs[a] = did("s", S.activation(T.sab[:, c], T.psa[:, o], F.Abs))
        need("s", k_col)
        k_scol[a] = did("s", S.activation(T.scol[:, a:a + 1], T.psb[:, 512 * a:512 * a + 1], F.Abs))

    def compare(a, lo, hi, op):
        need("v", k_scol[a], k_abs[hi - 1])
        return did("v", V.tensor_scalar(T.cmp[:, 512 * a + 128 * lo:512 * a + 128 * hi], T.sab[:, 128 * lo:128 * hi],
                                        T.scol[:, a:a + 1], None, op))

    def signs(a, lo, hi):
        need("s", k_scol[a], k_abs[hi - 1])
        return did("s", S.activation(T.sg[:, 512 * a + 128 * lo:512 * a + 128 * hi], T.sab[:, 128 * lo:128 * hi], F.Sign,
                                     bias=T.scol[:, a:a + 1], scale=-1.0))

    def tally(a, lo, hi, scale, k):
        c = slice(512 * a + 128 * lo, 512 * a + 128 * hi)
        need("s", k)
        return did("s", S.activation(T.junk[:, c], T.sg[:, c], F.Relu, scale=scale, accum_out=T.cn[:, a:a + 1]))

    def equal(a):
        c = slice(128 * a, 128 * a + 128)
        need("v", k_scol[a])
        return did("v", V.tensor_scalar(T.eqs[:, c], T.sab[:, c], T.scol[:, a:a + 1], -1.0, A.is_equal, A.mult))

    def ties(a, k):
        c = slice(128 * a, 128 * a + 128)
        need("v", k, k_off_p)
        return did("v", V.tensor_tensor_scan(T.tie[:, c], T.offp[:, :], T.eqs[:, c], 0.0, A.mult, A.add))

    def add_up(a, lo, hi, *toks):
        n, o = 64 * (hi - lo), 512 * a + 128 * lo
        need("v", *toks)
        return did("v", V.tensor_tensor_scan(T.scn[:, 256 * a + 256 - n:256 * a + 256], T.cmp[:, o:o + n],
                                             T.cmp[:, o + n:o + 2 * n], T.tie[:, 128 * a + 127:128 * a + 128], A.add, A.add))

    codes(0)
    need("v", k_u)
    k_uq = did("v", V.quantize_mx(T.uq[:, :], T.us[:, :], T.urep[:, :]))
    for a in (1, 2, 3):
        codes(a)
    for a in range(4):
        score(a)
    unit(0)
    unit(1)
    need("v", k_gi)
    k_gd = did("v", V.tensor_scalar(T.gd[:, :], T.gi[:, :], T.qf[:, 0:1], None, A.subtract))
    signs(0, 1, 3)
    k_sg = {0: signs(0, 3, 4), 1: signs(1, 2, 4)}
    k_up = {0: tally(0, 1, 4, -1.0, k_sg[0])}
    k_sg.update({2: signs(2, 3, 4), 3: signs(3, 0, 1)})
    k_up.update({1: tally(1, 2, 4, -1.0, k_sg[1]), 2: tally(2, 3, 4, -1.0, k_sg[2]), 3: tally(3, 0, 1, 1.0, k_sg[3])})
    span = {0: (0, 1), 1: (0, 2), 2: (0, 3), 3: (1, 4)}
    k_ge, k_same, k_tie = {}, {}, {}
    for a in (0, 1):
        k_ge[a], k_same[a] = compare(a, *span[a], A.is_ge), equal(a)
    for a in (0, 1):
        k_same[a + 2] = equal(a + 2)
        k_tie[a] = ties(a, k_same[a])
    k_ge[2] = compare(2, *span[2], A.is_ge)
    k_tie.update({2: ties(2, k_same[2]), 3: ties(3, k_same[3])})
    k_ge[3] = compare(3, *span[3], A.is_ge)
    k_sum = {a: add_up(a, *span[a], k_ge[a], k_tie[a]) for a in range(4)}
    for a in range(4):
        need("v", k_sum[a], k_up[a])
        last = (T.rof[:, a:a + 1], T.scn[:, 256 * a + 255:256 * a + 256], T.cn[:, a:a + 1])
        k_r = did("v", V.tensor_scalar(*last, None, A.add) if a < 3 else V.tensor_scalar(*last, 128.0, A.subtract, A.add))

    unit(2)
    need("v", k_r, k_win, k_gd)
    k_w = did("v", V.tensor_copy(T.win[:, 0:512].indirect(T.rof[:, 0:4]), T.gd[:, :]))
    unit(3)
    need("v", k_w, k_blk)
    did("v", V.tensor_copy(T.win2[:, :, 0:16], T.win[:, 0:128]))
    d2 = did("v", V.tensor_copy(T.win2[:, :, 16:32], T.win[:, 0:128]))
    did("v", V.tensor_scalar(T.b16[:, :], T.e32[:, 1:17], -2.0, None, A.mult))
    k_xo = did("v", V.tensor_scalar(T.xo[:, 0:1], T.blk[:, 0:1], 1.0 / 16, T.qf[:, 0:1], A.mult, A.add))
    need("v", d2)
    k_tr = did("v", V.transpose(T.tr[:, :, :], T.win2[:, :, :]))
    for i in (2, 3):
        k_mb = did("v", V.tensor_scalar(T.mb[:, i:i + 1], T.blk[:, 0:1], 128.0 * i, -4096.0, A.is_ge, A.mult))
    need("v", k_tr)
    k_a0 = did("v", V.tensor_tensor(T.a0[:, :], T.tr[:, :, 0], T.tr[:, :, 16], A.add))
    k_m16 = did("v", V.tensor_tensor(T.m16[:, :], T.e32[:, 0:16], T.b16[:, :], A.add))
    did("v", V.tensor_scalar(T.qf[:, 4:5], T.b16[:, 15:16], -1.0, -256.0, A.mult, A.add))
    need("v", k_a0)
    k_a1 = did("v", V.tensor_tensor(T.a1[0:64, :], T.a0[0:64, :], T.a0[64:128, :], A.add))
    need("v", k_a1)
    c = slice(8 * place[me], 8 * place[me] + 8)
    for b in range(4):
        k_lst = did("v", V.tensor_tensor(T.la[32 * b:32 * b + 32, c], T.a1[0:32, :], T.a1[32:64, :], A.add))
    need("v", k_lst)
    k_of = {}
    for t in (2, 0, 3, 1):
        k_of[t] = did("v", V.tensor_scalar(T.ofs[:, 8 * t:8 * t + 8], T.la[:, c], 4.0, 1024.0 + t, A.mult, A.add))
    k_sel = {}
    for t in (0, 1):
        need("v", k_of[t])
        k_sel[t] = did("v", V.tensor_copy(T.sel[:, t:512:4], T.grt[:, 0:2048].indirect(T.ofs[:, 8 * t:8 * t + 8])))
    k_sel[3] = did("v", V.tensor_copy(T.sel[:, 259:512:4], T.grt[:, 0:2048].indirect(T.ofs[:, 28:32])))
    for b in range(4):
        need("t", k_abs[3], k_eq[b])
        k = did("t", TE.matmul_mx(T.psa[:, 512 * b:512 * b + 512], T.eq[:, 128 * b:128 * b + 128],
                                  T.es[:, 128 * b:128 * b + 128], T.gq[:, :], T.gs[:, :], True, True))
        need("s", k)
        k_all = did("s", S.activation(T.dall[:, b:2048:4], T.psa[:, 512 * b:512 * b + 512], F.Copy, scale=-1.0))
    need("s", k_of[2])
    did("s", S.activation(T.sel[:, 2:512:4], T.grt[:, 0:2048].indirect(T.ofs[:, 16:24]), F.Copy))
    need("s", k_of[3])
    k_sel[2] = did("s", S.activation(T.sel[:, 3:256:4], T.grt[:, 0:2048].indirect(T.ofs[:, 24:28]), F.Copy))
    need("s", k_m16, k_qof, k_mb, k_num)
    k_mw = did("s", S.activation(T.mw[:, :], T.m16[:, 0:16].indirect(T.qof[:, :]), F.Copy))
    k_dat = did("s", S.activation(T.dat[:, :], T.num[:, 1:129], F.Identity, bias=T.blk[:, 0:1]))
    need("s", k_mw)
    for i in (2, 3):
        k_mp = did("s", S.activation(T.mp[:, 128 * i - 256:128 * i - 128], T.mw[:, 0:128], F.Identity,
                                     bias=T.mb[:, i:i + 1]))
    need("v", *k_sel.values())
    k_q = did("v", V.quantize_mx(T.qq[:, 0:128], T.pp[:, 0:128], T.sel[:, :]))

    sent = [0]

    def send(src, dst, sem, step=1):
        tr = []
        for c in plan:
            rid, pid, _ = topo.addr(c)
            slots, theirs = view_of(T.rank_of(c), T.cores, topo)
            use = plan[c][::step]
            tr.append(RemoteDMATransfer(dst_ids=[DstId(rid=rid, pnc=pid)], dma_engine_mask=sum(1 << e for e in use),
                                        remote_sem=T.sem[sem], src=src, dst=dst(128 * slots.index(me), theirs.index(me))))
            sent[0] += len(use)
        g.remote_dma_fused(tr, local_sem=T.sem.left)

    need("g", k_lst)
    send(T.la[:, c], lambda c, i: T.la[:, 8 * i:8 * i + 8], "al%d" % me)
    need("g", k_q)
    send(T.qq[:, 0:128].bitcast(dt.uint8), lambda c, i: T.qq[:, c:c + 128].bitcast(dt.uint8), "ac%d" % me)
    send(T.pp[:, 0:128], lambda c, i: T.pp[:, c:c + 128], "ac%d" % me)
    got = {s: ("ac%d" % s, 2 * narr[s]) for s in narr}
    heard = {s: ("al%d" % s, narr[s]) for s in narr}
    heard[me] = k_lst

    def decode(bank, lo, hi, *toks, rows=range(4)):
        need("t", *toks)
        return {b: did("t", TE.matmul_mx(bank[:, 512 * b:512 * b + hi - lo], T.eq[:, 128 * b:128 * b + 128],
                                         T.es[:, 128 * b:128 * b + 128], T.qq[:, lo:hi], T.pp[:, lo:hi], True, True))
                for b in rows}

    def region(i, b):
        return T.tab[:, b // G, G * (1 + 128 * i) + b % G:G * (129 + 128 * i):G]

    kept = {}

    def keep(s, bank, dec):
        for b in range(4):
            need("s", dec[b])
            kept[place[s], b] = did("s", S.activation(region(place[s], b), bank[:, 512 * b:512 * b + 128], F.Copy))

    dec = decode(T.psa, 0, 128, k_q, k_all)
    need("t", k_scol[3])
    k_sc = did("t", TE.matmul_mx(T.psb[:, 0:128], T.uq[:, :], T.us[:, :], T.qq[:, 0:128], T.pp[:, 0:128], True, True))
    k_dif = {}
    need("v", k_all)
    for b in range(4):
        k_dif[b] = did("v", V.tensor_tensor(T.dif[:, 128 * b:128 * b + 128],
                                            T.dall[:, 0:2048].indirect(T.ofs[:, 8 * b:8 * b + 8]), T.sel[:, b:512:4], A.add))
    k_ers = [k_er]

    def place_er(lo, hi):
        need("v", k_dif[hi - 1], *k_ers)
        k_ers[:] = [did("v", V.tensor_copy(T.er32[:, 0:2048].indirect(T.ofs[:, 8 * lo:8 * hi]),
                                           T.dif[:, 128 * lo:128 * hi]))]

    place_er(0, 1)
    keep(me, T.psa, dec)
    need("s", k_sc)
    k_scb = did("s", S.activation(T.scb[:, :], T.psb[:, 0:128], F.Abs))

    def unfold(out, src, pattern, *toks):
        need("v", *toks)
        return did("v", V.tensor_tensor_scan(out, src, pattern, -1024.0, A.max, A.add))

    def copy(q, out, src):
        return did(q, S.activation(out, src, F.Copy) if q == "s" else V.tensor_copy(out, src))

    def window(i, h):
        return T.tab[:, h, 0:G * (1 + 128 * i)].indirect(T.off[:, 8 * G * (i - 1):8 * G * i])

    def offsets(out, src, rows):
        return did("v", V.tensor_scalar(out, src, 1.0 * G, T.qf[rows, 4:5], A.mult, A.add))

    need("v", k_xo, *heard.values())
    k_xl = did("v", V.tensor_scalar(T.xl[:, :], T.la[:, 0:40].indirect(T.xo[:, 0:1]), 256.0, None, A.add))
    did("v", V.tensor_scalar(T.ll[:, :], T.la[:, 8:32], 256.0, None, A.add))
    place_er(1, 2)
    need("v", k_xl, k_pw, k_dat)
    k_en = did("v", V.tensor_copy(T.pw[:, 0:512].indirect(T.xl[:, 0:8]), T.dat[:, :]))
    place_er(2, 3)
    need("s", k_xl)
    k_nb = did("s", S.activation(T.nbl[:, :], T.num[:, 0:512].indirect(T.xl[:, 0:8]), F.Copy, bias=256.0))
    need("s", k_en)
    k_pv = did("s", S.activation(T.pv[:, 128:384], T.pw[:, 0:512].indirect(T.ll[:, 8:24]), F.Copy))
    need("v", k_en)
    k = did("v", V.tensor_copy(T.pv[:, 0:128], T.pw[:, 0:512].indirect(T.ll[:, 0:8])))
    unfold(T.un[:, 384:896], T.pw[:, :], T.mw[:, :], k_mw)
    k = unfold(T.un[:, 0:128], T.pv[:, 0:128], T.mw[:, 0:128], k)
    place_er(3, 4)
    need("v", k)
    first = slice(32 * order[0], 32 * order[0] + 32)
    for h in range(0, 128, 32):
        k_off1 = offsets(T.off[h:h + 32, 0:8 * G], T.un[first, R - 1:128:R], first)
    k = unfold(T.un[:, 128:384], T.pv[:, 128:384], T.mp[:, :], k_pv, k_mp)
    need("y", k_scb)
    ends = [dma("y", "stsc", T.sc[:, :], T.scb[0:1, :])]
    need("y", k_nb)
    ends.append(dma("y", "stnb", T.nb[:, :], T.nbl[0:128:32, :]))
    need("y", ("left", sent[0]), *k_ers)
    ends.append(dma("y", "ster", T.er[:, :], T.er32[:, :]))

    mine = list(kept.values())
    keep(mate, T.psb, decode(T.psb, 128, 256, got[mate], k_scb))
    theirs = list(kept.values())
    fetched, summed = {}, {}

    def fetch(q, h):
        need(q, k_off1, k_tab, kept[0, G * h + G - 1])
        fetched[h] = copy(q, T.gsum[:, h, :], window(1, h))

    def add(b):
        need("v", fetched[b // G], dx[b])
        summed[b // G] = did("v", V.tensor_tensor(region(1, b), T.gsum[:, b // G, b % G:128 * G:G],
                                                  T.psa[:, 512 * b:512 * b + 128], A.add))

    for h in range(1, 4 // G):
        fetch("s", h)
    dx, dy = {}, {}
    for rows in ((0, 1), (2, 3)):
        dx.update(decode(T.psa, 256, 384, got[x], *mine, rows=rows))
        dy.update(decode(T.psb, 384, 512, got[y], *theirs, rows=rows))
    keep(y, T.psb, dy)
    fetch("v", 0)
    need("v", k)
    k = did("v", V.tensor_tensor(T.c1[0:64, :], T.un[0:64, 127 + R:896:R], T.un[64:128, 127 + R:896:R], A.max))
    need("v", k)
    for h in (0, 32):
        k = did("v", V.tensor_tensor(T.c2[h:h + 32, :], T.c1[0:32, :], T.c1[32:64, :], A.max))
    add(0)
    add(1)
    need("v", k)
    for h in (0, 64):
        k_off = offsets(T.off[h:h + 64, 8 * G:56 * G], T.c2[0:64, :], slice(0, 64))
    add(2)
    add(3)

    for pair in ((0, 1), (2, 3)):
        for i, h in [(i, h) for i in (2, 3) for h in pair]:
            need("v", k_off, kept[i, G * h + G - 1], summed[h])
            o = T.tab[:, h, G * (1 + 128 * i):G * (129 + 128 * i)]
            summed[h] = did("v", V.tensor_tensor(o, window(i, h), o, A.add))

    edges = [sum(PIECES[:i]) for i in range(len(PIECES) + 1)]
    done = {i: [] for i in range(len(PIECES))}
    for q, h, i, j in GATHERS:
        lo, hi = edges[i], edges[j]
        need(q, summed[h])
        k = copy(q, T.accs[:, lo:hi, h],
                 T.tab[:, h, 0:513 * G].indirect(T.off[:, 24 * G + lo // R:24 * G + hi // R]))
        for n in range(i, j):
            done[n].append(k)
    for i in done:
        need("y", *done[i])
        lo, hi = edges[i], edges[i + 1]
        ends.append(dma("y", "sta%d" % i, T.acc[:, 4 * lo:4 * hi], T.accs[:, lo:hi, :]))

    need("y", *ends)
    need("g", ("left", sent[0]), *[(sem, count[sem]) for sem in ("gp", "ve", "se", "te")])
